import numpy as np, ml_dtypes
CORES = [242,247,114,119]
N = 4
BF = ml_dtypes.bfloat16
def gentries(a):
    return np.ascontiguousarray(a.reshape(8, 16, -1).transpose(0, 2, 1)).reshape(8, -1)
def gtable(e):
    e = np.asarray(e); return np.ascontiguousarray(e.reshape(8, -1, 16).transpose(0, 2, 1)).reshape(128, -1).astype(np.int32)
W, V, I, RO = 2048, 1024, 256, 4
P = V // I
def parts(rng):
    return (rng.integers(0, W, (N, 8, 16, W)), rng.integers(0, 256, (N, 8, 16, V)), rng.integers(0, 256, (N, 8, 16, I)),
            rng.integers(0, W, (N, 8, I)), rng.integers(0, 256, (N, 8, 16)))
def pack(S, X, x, s, w):
    return {"stm": np.ascontiguousarray(S.reshape(N, 128, W)).astype(np.int32), "vx": X.reshape(N, 128, V).astype(np.float32).astype(BF),
            "x0": x.reshape(N, 128, I).astype(np.float32).astype(BF), "s0": np.stack([gtable(a) for a in s]), "wt": w.reshape(N, 128, 1).astype(np.int32)}
def two(rng, lo, hi, shape):
    return np.where(rng.random(shape) < 0.5, lo, hi)
def tame(rng, S, w, cl):
    col = np.arange(W); ev = col[((col >> 4) & 1) == 0]
    off = np.where(cl, 0, rng.integers(1, 16, cl.shape))
    S[:, ev] = 32 * np.argsort(rng.random((16, W // 32, 16)), axis=1).reshape(16, W // 2) + 16 + ((ev + off) & 15)
    w[:] = 32 * rng.integers(1, 8, 16)
    return ev
def lay(rng, S, w, cl, no):
    off = rng.integers(1, 15, cl.shape); off = np.where(cl, 0, off + (off >= 16 - no))
    S[:] = 16 * rng.integers(0, W // 16, cl.shape) + ((np.arange(W) + off) & 15)
    w[:] = 32 * rng.integers(1, 8, 16)
def wake(S, X, w, k, c):
    if (S[k, c] & (V - 1)) == (S[k ^ 1, c] & (V - 1)): S[k ^ 1, c] = S[k ^ 1, c] ^ 16
    a = S[k, c] & (V - 1); b = S[k ^ 1, c] & (V - 1)
    X[0, b] = X[0, a] ^ 1
    if int(np.add.reduce(w * np.abs(X[:, a] - X[:, b]))) & (W - 1) == 0: w[0] = w[0] ^ 32
def setup_inputs(rng):
    return pack(*parts(rng))
def setup_inputs_corners(rng):
    S, X, x, s, w = parts(rng); M = W // 2; role = rng.permutation(N)
    for q in range(N):
        kinds = rng.permutation(8); gx = int(rng.integers(0, 8))
        for g in range(8):
            kind = int(kinds[g])
            if role[q] == 0 or role[q] == 2: kind = 0 if g % 2 == 0 else 2
            if role[q] == 1: kind = 1
            if role[q] == 2 and g == gx: kind = 8
            if kind == 6:
                S[q, g] = np.arange(W)[None, :]; s[q, g, 0] = W - 1; s[q, g, I - 1] = 0; continue
            if kind == 7:
                s[q, g] = two(rng, 0, W - 1, I); continue
            cl = np.zeros((16, M), bool); p = rng.permutation(M)
            if kind == 1: cl[:] = True
            if kind == 2: cl[15] = True
            if kind == 3: cl[0] = True; cl[15] = True
            if kind == 4: cl[14:] = rng.random(M) < 0.5
            if kind == 5: cl = np.argsort(rng.random((16, M)), axis=0) < rng.integers(0, 17, M)
            if kind == 8:
                n = int(rng.integers(15, 18)); cl[3, p[:n]] = True; cl[9, p[:n]] = True
            ev = tame(rng, S[q, g], w[q, g], cl)
            s[q, g] = rng.permutation(ev[p[:I]])
    return pack(S, X, x, s, w)
def setup_inputs_late(rng):
    S, X, x, s, w = parts(rng); odd = int(rng.integers(0, 2)); col = np.arange(W)
    for q in range(N):
        if q % 2 == odd:
            al = int(rng.integers(1, 16)); n = 16 * int(rng.integers(I // 16, 5 * I // 16)) + al
            fk = rng.permutation(8 * (I - 1)).reshape(8, I - 1) < n
            for g in range(8):
                m = np.where((col & 1) == 1, rng.integers(0, 2, W), rng.integers(2, 5, W)); m[W - 1] = 0
                lay(rng, S[q, g], w[q, g], np.argsort(rng.random((16, W)), axis=0) < m, al)
                s[q, g] = 2 * rng.integers(0, W // 2, I) + 1; s[q, g, :I - 1] -= fk[g].astype(np.int64); s[q, g, I - 1] = W - 1
            continue
        kinds = rng.permutation(8)
        for g in range(8):
            kind = int(kinds[g]) // 2; Sg, Xg, wg = S[q, g], X[q, g], w[q, g]
            if kind == 3: continue
            no = int(rng.integers(1, 16)); e = 16 * (1 + rng.permutation(W // 16 - 1)[:4])
            if kind == 0:
                lay(rng, Sg, wg, np.zeros((16, W), bool), no)
                k = int(rng.integers(0, 16)); c = int(rng.integers(0, W)); at = np.arange(c & 15, W, 16)
                Sg[k, at] = c; s[q, g] = rng.choice(at, I); wake(Sg, Xg, wg, k, c); continue
            lay(rng, Sg, wg, rng.random((16, W)) < 0.0625, no)
            if kind == 1:
                Sg[Sg == 0] = 16
                Sg[0, e[0]] = 0; Sg[0, e[1]] = 5; Sg[1, e[1]] = 0
                s[q, g, 0] = e[0]; s[q, g, 1] = e[1]; wake(Sg, Xg, wg, 0, 0)
            if kind == 2:
                ka = int(rng.integers(0, 15)); kb = int(rng.integers(ka + 1, 16))
                Sg[:, e] = 16 * rng.integers(0, W // 16, (16, 4)) + rng.integers(1, 16, (16, 4))
                Sg[ka, e] = 16 * rng.integers(1, W // 16, 4); Sg[kb, e] = 0
                z = np.abs(Xg[:, Sg[kb, 0] & (V - 1)] - Xg[:, Sg[kb ^ 1, 0] & (V - 1)])
                s[q, g, 1::2] = rng.choice(e, I // 2); x[q, g, :, 1::2] = z[:, None]
    return pack(S, X, x, s, w)
def setup_inputs_ties(rng):
    S, X, x, s, w = parts(rng)
    pool = np.argsort(rng.random((N, 8, W)), axis=-1)[..., :32]; pool[..., 0] = W - 1; pool[..., 1] = 0
    S = np.take_along_axis(pool[:, :, None, :], rng.integers(0, 32, (N, 8, 16, W)), 3)
    s = np.take_along_axis(pool, rng.integers(0, 32, (N, 8, I)), 2)
    few = np.take_along_axis(X[..., :5], rng.integers(0, 5, (N, 8, 1, V)), 3)
    X[:, ::2] = few[:, ::2]; x[:, 1::2] = x[:, 1::2, :, :1]
    return pack(S, X, x, s, w)
def setup_inputs_ends(rng):
    S, X, x, s, w = parts(rng)
    S = np.where(rng.random(S.shape) < 0.7, two(rng, 0, W - 1, S.shape), S)
    S[..., 0] = two(rng, 0, W - 1, (N, 8, 16)); S[..., W - 1] = two(rng, 0, W - 1, (N, 8, 16))
    S[:, :, [0, 1, 14, 15], 0] = np.array([0, W - 1, 0, W - 1]); S[:, :, [0, 1, 14, 15], W - 1] = np.array([0, W - 1, W - 1, 0])
    S[:, :, 4:6, 0] = 0; S[:, :, 4:6, W - 1] = W - 1
    q = 16 * rng.integers(1, W // 16 - 1, (N, 8)); S[:, :, 2, 0] = q; S[:, :, 2, W - 1] = q + 15
    for a in range(N):
        for g in range(8):
            S[a, g, 2:4, q[a, g]] = W - 1; S[a, g, 2:4, q[a, g] + 15] = 0
    S[:, :, 1, W - 2] = W - 1; S[:, :, 15, W - 2] = W - 1
    X = two(rng, 0, 255, X.shape); X[..., 0] = 0; X[..., V - 1] = 255
    x = two(rng, 0, 255, x.shape); w = two(rng, 0, 255, w.shape)
    w[:, 0] = 255; w[:, 7] = 255; w[:, 1::5] = 0; w[:, 1::5, 15] = 255; w[:, 1::5, 14] = 2
    s = np.where(rng.random(s.shape) < 0.8, two(rng, 0, W - 1, s.shape), s); s[N - 1] = two(rng, 0, W - 1, (8, I))
    s[:, 7, I - 1] = W - 1; s[:, 0, 2] = W - 1; s[:, 7, 1] = 0
    s[:, 1::5, 3] = W - 2; s[:, 1::5, I - 1] = W - 2; s[:, 1::5, I - 2] = W - 1; s[:, 1::5, 4] = W - 1
    return pack(S, X, x, s, w)
def setup_inputs_spread(rng):
    S, X, x, s, w = parts(rng)
    p = rng.choice(np.array([1.0, 1.5, 2.0, 4.0]), (N, 8, 1, 1)); fl = rng.random((N, 8, 1, 1)) < 0.5
    S = np.minimum((W * rng.random(S.shape) ** p).astype(np.int64), W - 1); S = np.where(fl, W - 1 - S, S)
    s = np.minimum((W * rng.random(s.shape) ** p[..., 0]).astype(np.int64), W - 1)
    X = np.minimum((np.exp2(8 * rng.random((N, 8, 1, V))) * rng.random(X.shape)).astype(np.int64), 255)
    x = np.minimum((np.exp2(8 * rng.random((N, 8, 1, I))) * rng.random(x.shape)).astype(np.int64), 255)
    w = np.minimum(np.exp2(8 * rng.random(w.shape)).astype(np.int64), 255)
    return pack(S, X, x, s, w)
def check_inputs(d):
    bad = []
    for k, lo, hi in (("stm", 0, W - 1), ("vx", 0, 255), ("x0", 0, 255), ("s0", 0, W - 1), ("wt", 0, 255)):
        v = np.asarray(d[k]).astype(np.float64)
        if not (np.min(v) >= lo and np.max(v) <= hi): bad.append("range of " + k)
        elif np.any(v != np.floor(v)): bad.append("whole numbers in " + k)
    return bad
def reference(stm, vx, x0, s0, wt):
    S = stm.astype(np.int64).reshape(N, 8, 16, W); X = vx.astype(np.float32).astype(np.int64).reshape(N, 8, 16, V)
    x = x0.astype(np.float32).astype(np.int64).reshape(N, 8, 16, I); w = wt.astype(np.int64).reshape(N, 8, 16, 1, 1)
    s = np.stack([gentries(a) for a in s0]).astype(np.int64)
    A = np.zeros(N, np.int64); mate = np.arange(16) ^ 1
    for t in range(RO):
        c = np.take_along_axis(S, s[:, :, None, :], 3)
        a = np.take_along_axis(S, c, 3) & (V - 1); b = np.take_along_axis(S[:, :, mate], c, 3) & (V - 1)
        z = np.abs(np.take_along_axis(X, a.reshape(N, 8, 1, 16 * I), 3) - np.take_along_axis(X, b.reshape(N, 8, 1, 16 * I), 3)).reshape(N, 8, 16, 16, I)
        u = np.add.reduce(w * z, axis=2) & (W - 1)
        claim = ((((u * u) >> 5) + u + c + A[:, None, None, None]) & 15) == (s & 15)[:, :, None, :]
        n = np.add.accumulate(claim.astype(np.int64), axis=2)
        has = n[:, :, 15] >= 1; fork = n[:, :, 15] >= 2
        k1 = np.argmax(claim & (n == 1), axis=2); k2 = np.argmax(claim & (n == 2), axis=2)
        c1 = np.take_along_axis(c, k1[:, :, None, :], 2)[:, :, 0]; c2 = np.take_along_axis(c, k2[:, :, None, :], 2)[:, :, 0]
        u1 = np.take_along_axis(u, k1[:, :, None, :], 2)[:, :, 0]
        z1 = np.take_along_axis(z, k1[:, :, None, None, :], 3)[:, :, :, 0]; z2 = np.take_along_axis(z, k2[:, :, None, None, :], 3)[:, :, :, 0]
        h = 1 + t % (N - 1)
        came = np.roll(fork, h, axis=0); cc = np.roll(c2, h, axis=0); cx = np.roll(np.abs(x - z2), h, axis=0)
        s = np.where(has, c1, np.where(came, cc, (5 * s + u[:, :, 0]) & (W - 1)))
        x = np.where(has[:, :, None], (x + z1) >> 1, np.where(came[:, :, None], cx, x))
        for r in range(N):
            for g in range(8):
                i = np.flatnonzero(has[r, g])
                X[r, g][:, P * i + (u1[r, g, i] & (P - 1))] = z1[r, g][:, i]
                col, at = np.unique(c1[r, g, i], return_index=True)
                i = i[at]; k = k1[r, g, i]
                S[r, g, k, col] = (S[r, g, k, col] + u1[r, g, i]) & (W - 1)
        A = np.add.reduce(fork.astype(np.int64), axis=(1, 2)) & 15
    return {"yt": np.add.reduce(S.reshape(N, 128, W // 256, 256), axis=2).astype(np.float32), "yv": X.reshape(N, 128, V).astype(np.float32).astype(BF),
            "yx": x.reshape(N, 128, I).astype(np.float32).astype(BF), "ys": np.stack([gtable(e) for e in s]).astype(np.float32)}

@@ -1,0 +1,464 @@
+from concourse.mybir import AluOpType as A, AxisListType, ActivationFunctionType as F
+
+STEPS, W, V, I = 4, 2048, 1024, 256
+CHUNKS = [64, 64, 64, 64]
+DUMP = 256
+XB0 = 8192
+BIG = 4096.0
+HALF = 1023.5
+M2K = 25769803776.0
+MAGIC = 12582912.0
+
+SCRATCH = {
+    "S": ("sbuf", [128, DUMP + W], "int32"),
+    "X": ("sbuf", [128, XB0 + 2 * V], "bfloat16"),
+    "G": ("sbuf", [128, 4096], "float16"),
+    "XB": ("sbuf", [128, 4096], "bfloat16"),
+    "D": ("sbuf", [128, 4096], "bfloat16"),
+    "Z": ("sbuf", [128, 4096], "bfloat16"),
+    "EQ": ("sbuf", [128, 4096], "float16"),
+    "c16": ("sbuf", [128, 256], "uint16"),
+    "lab": ("sbuf", [128, 512], "uint16"),
+    "c16p": ("sbuf", [128, 256], "float16"),
+    "sq": ("sbuf", [128, 256], "float32"),
+    "N1": ("sbuf", [128, 256], "float32"),
+    "uq": ("sbuf", [128, 256], "float32"),
+    "uh": ("sbuf", [128, 256], "float16"),
+    "Qi": ("sbuf", [128, 256], "int32"),
+    "Qa": ("sbuf", [128, 256], "int32"),
+    "cl": ("sbuf", [128, 256], "float16"),
+    "H2c": ("sbuf", [128, 256], "float16"),
+    "F1c": ("sbuf", [128, 256], "float16"),
+    "F1u": ("sbuf", [128, 256], "float16"),
+    "SF": ("sbuf", [128, 512], "bfloat16"),
+    "R1": ("sbuf", [128, 256], "float16"),
+    "cnr": ("sbuf", [128, 256], "bfloat16"),
+    "zz": ("sbuf", [128, 512], "bfloat16"),
+    "nc": ("sbuf", [128, 256], "int32"),
+    "nd": ("sbuf", [128, 256], "int32"),
+    "XF": ("sbuf", [128, 256], "bfloat16"),
+    "yto": ("sbuf", [128, 256], "float32"),
+    "c1L": ("sbuf", [128, 16], "float32"), "cl16": ("sbuf", [128, 16], "uint16"), "zo16": ("sbuf", [128, 32], "uint16"),
+    "gl": ("sbuf", [128, 16], "float32"), "gs": ("sbuf", [128, 1], "float32"), "Ai": ("sbuf", [128, 1], "int32"),
+    "Aj": ("sbuf", [128, 1], "int32"), "Af": ("sbuf", [128, 1], "float32"),
+    "ux": ("sbuf", [128, 16], "int32"), "uy": ("sbuf", [128, 16], "int32"), "xo": ("sbuf", [128, 16], "float32"),
+    "xo16": ("sbuf", [128, 16], "uint16"), "so": ("sbuf", [128, 16], "float32"), "so16": ("sbuf", [128, 16], "uint16"),
+    "si5": ("sbuf", [128, 16], "float32"), "w1": ("sbuf", [128, 16], "int32"), "w2": ("sbuf", [128, 16], "int32"),
+    "w3": ("sbuf", [128, 16], "float32"), "b0": ("sbuf", [128, 16], "float32"), "b1": ("sbuf", [128, 16], "float32"),
+    "vi": ("sbuf", [128, 16], "int32"), "si": ("sbuf", [128, 16], "int32"), "sl16": ("sbuf", [128, 16], "uint16"),
+    "sx": ("sbuf", [128, 16], "int32"), "sy": ("sbuf", [128, 16], "float32"), "sel16": ("sbuf", [128, 16], "uint16"),
+    "sA": ("sbuf", [128, 16], "float16"), "yso": ("sbuf", [128, 16], "float32"),
+    "onesb": ("sbuf", [128, 128], "bfloat16"), "mones": ("sbuf", [128, 128], "float32"),
+    "Ib": ("sbuf", [128, 128], "bfloat16"), "Jb": ("sbuf", [128, 128], "bfloat16"), "blk": ("sbuf", [128, 128], "bfloat16"),
+    "tr": ("sbuf", [128, 128], "bfloat16"), "Y1": ("sbuf", [128, 128], "bfloat16"), "Y2": ("sbuf", [128, 128], "bfloat16"),
+    "Q1": ("sbuf", [128, 128], "bfloat16"), "Q2": ("sbuf", [128, 128], "bfloat16"), "I32": ("sbuf", [128, 128], "bfloat16"),
+    "L0": ("sbuf", [128, 2048], "bfloat16"), "cF": ("sbuf", [128, 256], "float16"), "c1h": ("sbuf", [128, 16], "float16"), "Ih": ("sbuf", [128, 128], "bfloat16"), "In": ("sbuf", [128, 128], "bfloat16"),
+    "Ea": ("sbuf", [128, 2048], "bfloat16"), "Eb": ("sbuf", [128, 2048], "bfloat16"), "Wm": ("sbuf", [128, 2048], "bfloat16"),
+    "L": ("sbuf", [128, 2048], "bfloat16"), "LK": ("sbuf", [128, 2048], "bfloat16"), "LK2": ("sbuf", [128, 2048], "bfloat16"),
+    "Lp": ("sbuf", [128, 2048], "bfloat16"), "Tr": ("sbuf", [128, 2048], "bfloat16"), "Lq": ("sbuf", [128, 2048], "bfloat16"),
+    "Tq": ("sbuf", [128, 2048], "bfloat16"),
+    "cB": ("sbuf", [128, 256], "bfloat16"), "cQ": ("sbuf", [128, 256], "bfloat16"),
+    "khi": ("sbuf", [128, 32], "bfloat16"), "klo": ("sbuf", [128, 32], "bfloat16"),
+    "pi": ("sbuf", [128, 1], "int32"), "pa": ("sbuf", [128, 1], "int32"), "pg": ("sbuf", [128, 1], "int32"),
+    "p15": ("sbuf", [128, 1], "float32"), "pgf": ("sbuf", [128, 1], "float32"), "k0": ("sbuf", [128, 1], "float32"),
+    "kc": ("sbuf", [128, 1], "float32"), "kc2": ("sbuf", [128, 1], "float32"), "kl": ("sbuf", [128, 1], "float32"),
+    "cg": ("sbuf", [128, 128], "float32"), "kk": ("sbuf", [128, 16], "float32"), "K16": ("sbuf", [128, 16], "float32"),
+    "i16": ("sbuf", [128, 16], "float32"), "il": ("sbuf", [128, 16], "float32"), "i4": ("sbuf", [128, 16], "float32"),
+    "ip": ("sbuf", [128, 16], "float32"), "wi": ("sbuf", [128, 1], "int32"), "wf": ("sbuf", [128, 1], "float32"),
+}
+for _t in range(STEPS):
+    SCRATCH["XW%d" % _t] = ("sbuf", [128, 8192 + 256], "bfloat16")
+    SCRATCH["ns%d" % _t] = ("sbuf", [128, 16], "float32")
+    SCRATCH["na%d" % _t] = ("sbuf", [128, 16], "float32")
+    SCRATCH["xs%d" % _t] = ("sbuf", [128, 256], "bfloat16")
+for _b in range(8):
+    SCRATCH["P%d" % _b] = ("psum", [128, 512], "float32")
+SEMAPHORES = ["qV", "qS", "qP", "qG", "loc"] + ["aN%d" % t for t in range(STEPS)] + ["aX%d" % t for t in range(STEPS)] + ["d%d" % j for j in range(12)]
+
+
+def rank_program(g, core, T, topo):
+    rank = T.rank_of(core)
+    if rank is None:
+        return
+    eng = {"V": g.vector, "S": g.scalar, "P": g.tensor, "G": g, "Y": g.sync}
+    cnt = {"V": 0, "S": 0, "P": 0, "G": 0, "D": 0, "loc": 0}
+    known = {q: {} for q in eng}
+    rec = {}
+    psum = {"P%d" % b for b in range(8)}
+    totals = {}
+
+    def need(q, ev):
+        k = known[q]
+        if k.get(ev[0], 0) < ev[1]:
+            eng[q].wait_ge(T.sem[ev[0]], ev[1])
+            for s, v in ev[3].items():
+                if k.get(s, 0) < v:
+                    k[s] = v
+            k[ev[0]] = ev[1]
+
+    def deps(q, dma, reads, writes):
+        out = []
+        for n, a, b in reads:
+            for (c, d, ev, kind) in rec.get(n, ()):
+                if n in psum:
+                    if ev[2] != q:
+                        out.append(ev)
+                elif kind == "w" and c < b and a < d:
+                    out.append(ev)
+        for n, a, b in writes:
+            for (c, d, ev, kind) in rec.get(n, ()):
+                if n in psum:
+                    if ev[2] != q:
+                        out.append(ev)
+                elif c < b and a < d and (kind == "w" or ev[2] != q):
+                    out.append(ev)
+        best = {}
+        for ev in out:
+            if ev[0] not in best or best[ev[0]][1] < ev[1]:
+                best[ev[0]] = ev
+        for ev in best.values():
+            need(q, ev)
+
+    def note(ev, reads, writes):
+        for n, a, b in writes:
+            if n in psum:
+                rec[n] = [(0, 512, ev, "w")]
+            else:
+                rec[n] = [r for r in rec.get(n, []) if not (a <= r[0] and r[1] <= b)] + [(a, b, ev, "w")]
+        for n, a, b in reads:
+            if n in psum:
+                rec[n] = [(0, 512, ev, "w")]
+            else:
+                rec[n] = [r for r in rec.get(n, []) if not (r[3] == "r" and r[2][2] == ev[2] and a <= r[0] and r[1] <= b)] + [(a, b, ev, "r")]
+
+    def emit(q, calls, reads, writes):
+        deps(q, False, reads, writes)
+        last = None
+        for c in calls:
+            last = c()
+        cnt[q] += 1
+        last.then_inc(T.sem["q" + q], 1)
+        totals["q" + q] = cnt[q]
+        note(("q" + q, cnt[q], q, dict(known[q])), reads, writes)
+
+    def dma(q, out, in_, reads, writes):
+        deps(q, True, reads, writes)
+        s = "d%d" % cnt["D"]
+        cnt["D"] += 1
+        eng[q].dma_start(out, in_).then_inc(T.sem[s], 16)
+        totals[s] = 16
+        note((s, 16, "D", dict(known[q])), reads, writes)
+
+    def v(n, a=None, b=None, step=1):
+        if a is None:
+            a, b = 0, T[n].shape[-1]
+        ap = T[n][:, a:b] if step == 1 else T[n][:, a:b:step]
+        return (ap, [(n, a, b)])
+
+    def row(n, b):
+        return (T[n][0:1, 0:b], [(n, 0, b)])
+
+    def ind(win, off):
+        return (win[0].indirect(off[0]), win[1], off[1])
+
+    def split(x):
+        return x[1] + (x[2] if len(x) > 2 else [])
+
+    def copy(out, in_):
+        emit("V", [lambda: g.vector.tensor_copy(out=out[0], in_=in_[0])], split(in_) + (out[2] if len(out) > 2 else []), out[1])
+
+    def tt(out, a, b, op):
+        emit("V", [lambda: g.vector.tensor_tensor(out=out[0], in0=a[0], in1=b[0], op=op)], split(a) + split(b), out[1])
+
+    def ts(out, a, s1, op0, s2=None, op1=None):
+        rd = split(a)
+        x1, x2 = s1, s2
+        if isinstance(s1, tuple):
+            rd = rd + s1[1]; x1 = s1[0]
+        if isinstance(s2, tuple):
+            rd = rd + s2[1]; x2 = s2[0]
+        if op1 is None:
+            emit("V", [lambda: g.vector.tensor_scalar(out=out[0], in0=a[0], scalar1=x1, scalar2=None, op0=op0)], rd, out[1])
+        else:
+            emit("V", [lambda: g.vector.tensor_scalar(out=out[0], in0=a[0], scalar1=x1, scalar2=x2, op0=op0, op1=op1)], rd, out[1])
+
+    def fill(out, c):
+        emit("V", [lambda: g.vector.memset(out[0], c)], [], out[1])
+
+    def act(out, in_, f, scale=1.0, bias=0.0):
+        rd = split(in_)
+        sc = scale
+        if isinstance(scale, tuple):
+            rd = rd + scale[1]; sc = scale[0]
+        emit("S", [lambda: g.scalar.activation(out=out[0], in_=in_[0], func=f, bias=bias, scale=sc)], rd, out[1])
+
+    def mms(items):
+        calls, rd, wr = [], [], []
+        for o, l, r, a, b in items:
+            calls.append(lambda o=o, l=l, r=r, a=a, b=b: g.tensor.matmul(o[0], l[0], r[0], a, b))
+            rd = rd + [x for x in l[1] + r[1] if x not in rd]
+            wr = wr + [x for x in o[1] if x not in wr]
+        emit("P", calls, rd, wr)
+
+    def iota(out, pattern, base, cm, flag=True):
+        emit("G", [lambda: g.iota(out[0], pattern, base, cm, allow_small_or_imprecise_dtypes=flag)], [], out[1])
+
+    def asel(out, in_, pattern, op, base, cm):
+        emit("G", [lambda: g.affine_select(out[0], in_[0], pattern, op, 0.0, base, cm)], in_[1], out[1])
+
+    def m16(n, r):
+        return v(n, 128 * r, 128 * r + 128)
+
+    dma("Y", T.si[:], T.s0[:], [], [("si", 0, 16)])
+    dma("S", T.S[:, DUMP + 1024:DUMP + 2048], T.stm[:, 1024:2048], [], [("S", DUMP + 1024, DUMP + 2048)])
+    dma("Y", T.S[:, DUMP:DUMP + 1024], T.stm[:, 0:1024], [], [("S", DUMP, DUMP + 1024)])
+    dma("Y", T.wi[:], T.wt[:], [], [("wi", 0, 1)])
+    dma("Y", T.X[:, XB0:XB0 + V], T.vx[:], [], [("X", XB0, XB0 + V)])
+    dma("Y", T.X[:, XB0 + V:XB0 + 2 * V], T.vx[:], [], [("X", XB0 + V, XB0 + 2 * V)])
+    dma("Y", T.XW0[:, 0:256], T.x0[:], [], [("XW0", 0, 256)])
+
+    iota(v("pi"), [[0, 1]], 0, 1, False)
+    fill(v("onesb"), 1.0)
+    fill(v("L"), 0.0)
+    fill(v("cB"), -BIG)
+    fill(v("Lq"), -32.0)
+    iota(v("cg"), [[1, 8], [0, 16]], 0, 0)
+    iota(v("kk"), [[1, 16]], 0, 0)
+    asel(v("Ib"), v("onesb"), [[-1, 128]], A.is_equal, 0, 1)
+    asel(v("Jb"), v("onesb"), [[-2, 64], [1, 2]], A.is_equal, -1, 1)
+    ts(v("pa"), v("pi"), 15, A.bitwise_and)
+    ts(v("pg"), v("pi"), 4, A.arith_shift_right)
+    copy(v("p15"), v("pa"))
+    copy(v("pgf"), v("pg"))
+    ts(v("blk"), v("cg"), v("pgf"), A.is_equal)
+    ts(v("K16"), v("kk"), v("p15"), A.is_equal)
+    copy(v("sl16"), v("si"))
+    for k in range(16):
+        ts(m16("Ea", k), v("Ib"), v("K16", k, k + 1), A.mult)
+        ts(m16("Eb", k), v("Jb"), v("K16", k ^ 1, (k ^ 1) + 1), A.mult)
+    for r in range(16):
+        act(v("L", 128 * r + r, 128 * r + 128, 16), v("blk", r, 128, 16), F.Copy)
+    iota(v("i16"), [[16, 16]], 0, 0)
+    iota(v("khi"), [[0, 2], [256, 16]], 0, 0)
+    asel(v("tr"), v("blk"), [[1, 128]], A.is_gt, 0, -1)
+    asel(v("Lp"), v("Lq"), [[-1, 16], [-16, 8], [0, 16]], A.is_equal, 0, 1)
+    fill(v("Tq"), 1.0)
+    asel(v("Tr"), v("Tq"), [[1, 16], [16, 8], [0, 16]], A.is_ge, -1, -1)
+    asel(v("Tq"), v("Tr"), [[0, 16], [-16, 8], [0, 16]], A.is_ge, 0, 1)
+    copy(v("wf"), v("wi"))
+    act(v("Wm"), v("L"), F.Copy, v("wf"))
+    ts(v("k0"), v("p15"), 0.0, A.is_equal)
+    ts(v("kc"), v("p15"), 1.0, A.add, 1.0 / 8192, A.mult)
+    ts(v("kc2"), v("kc"), -2.0, A.mult)
+    ts(v("kl"), v("p15"), 16.0, A.mult, -1.0, A.add)
+    ts(v("il"), v("i16"), v("p15"), A.add)
+    ts(v("i4"), v("il"), 4.0, A.mult)
+    ts(v("ip"), v("il"), -255.0, A.add)
+    ts(v("cF"), v("cB"), 0.0, A.mult, -HALF, A.add)
+    act(v("L0"), v("L"), F.Copy, v("k0"))
+    ts(v("klo"), v("khi"), 0.0, A.mult, v("kl"), A.add)
+    tt(v("Y1"), v("Ib"), v("tr"), A.subtract)
+    tt(v("Y2"), v("Y1"), v("Ib"), A.add)
+    fill(v("Af"), 0.0)
+    fill(v("mones"), -1.0)
+    fill(v("cQ"), -0.25)
+    act(v("I32"), v("Ib"), F.Copy, 32.0)
+    act(v("Ih"), v("Ib"), F.Copy, 0.5)
+    act(v("In"), v("Ib"), F.Copy, -1.0)
+    act(v("Q1"), v("Y1"), F.Copy, BIG)
+    act(v("Q2"), v("Y2"), F.Copy, BIG)
+    act(v("LK"), v("L"), F.Copy, v("kc"))
+    act(v("LK2"), v("L"), F.Copy, v("kc2"))
+
+    Sw = v("S", DUMP, DUMP + W)
+    Xw = v("X", XB0, XB0 + 2 * V)
+    starts = [sum(CHUNKS[:j]) for j in range(len(CHUNKS) + 1)]
+    later_v, later_s = [], []
+
+    def lists(bank, a, n, mat, src, s0, s1, start=True, stop=True):
+        mms([(v(bank, a, a + n), m16(mat, r), v(src, s0 + r, s1, 16), start and r == 0, stop and r == 15) for r in range(16)])
+
+    for t in range(STEPS):
+        last = t == STEPS - 1
+        h = 1 + t % 3
+        XW = "XW%d" % t
+        copy(v("c16"), ind(Sw, v("sl16")))
+
+        def gath(j):
+            i0, i1 = starts[j], starts[j + 1]
+            copy(v("G", 16 * i0, 16 * i1), ind(Sw, v("c16", i0, i1)))
+
+        def sel(j):
+            i0, i1 = starts[j], starts[j + 1]
+            n = i1 - i0
+            b = "P%d" % (j % 2)
+            mms([(v(b, n, 2 * n), m16("Eb", k), v("G", 16 * i0 + k, 16 * i1, 16), k == 0, k == 15) for k in range(16)])
+            mms([(v(b, 0, n), m16("Ea", k), v("G", 16 * i0 + k, 16 * i1, 16), k == 0, k == 15) for k in range(16)])
+
+        def conv(j):
+            i0, i1 = starts[j], starts[j + 1]
+            copy(v("lab", 2 * i0, 2 * i1), v("P%d" % (j % 2), 0, 2 * (i1 - i0)))
+            act(v("XB", 16 * i0, 16 * i1), ind(Xw, v("lab", i0 + i1, 2 * i1)), F.Copy)
+
+        def diff(j):
+            i0, i1 = starts[j], starts[j + 1]
+            tt(v("D", 16 * i0, 16 * i1), ind(Xw, v("lab", 2 * i0, i0 + i1)), v("XB", 16 * i0, 16 * i1), A.subtract)
+            act(v("Z", 16 * i0, 16 * i1), v("D", 16 * i0, 16 * i1), F.Abs)
+            mms([(v("P2", i0, i1), m16("Wm", k), v("Z", 16 * i0 + k, 16 * i1, 16), False, k == 15 and i1 == I) for k in range(16)])
+
+        gath(0)
+        sel(0)
+        ts(v("c16p"), v("c16"), 1.0, A.add)
+        for f in later_v:
+            f()
+        ts(v("sA"), v("si"), v("Af"), A.subtract, 7.0, A.subtract)
+        gath(1)
+        sel(1)
+        conv(0)
+        for f in later_s:
+            f()
+        gath(2)
+        sel(2)
+        conv(1)
+        mms([(v("P2", 0, 256), row("onesb", 128), row("cF", 256), True, False)])
+        mms([(v("P3", 0, 256), v("I32"), v("c16p"), True, False)] +
+            [(v("P3", r, 256, 16), m16("Lp", r), v("sA"), False, r == 15) for r in range(16)])
+        mms([(v("P4", 0, 256), v("Ib"), v("c16p"), True, False), (v("P4", 0, 256), row("onesb", 128), row("cB", 256), False, False)])
+        mms([(v("P5", 0, 256), v("Ib"), v("c16p"), True, False)])
+        gath(3)
+        sel(3)
+        conv(2)
+        diff(0)
+        conv(3)
+        diff(1)
+        diff(2)
+        diff(3)
+        ts(v("N1"), v("P2", 0, 256), M2K, A.add, M2K, A.subtract)
+        tt(v("uq"), v("P2", 0, 256), v("N1"), A.subtract)
+        act(v("sq"), v("uq"), F.Square, 1.0, HALF + 16.0)
+        ts(v("uh"), v("uq"), HALF, A.add)
+        mms([(v("P2", 0, 256), v("Ib"), v("uh"), True, False)])
+        tt(v("Qi"), v("sq"), v("P3", 0, 256), A.add)
+        ts(v("Qa"), v("Qi"), 480, A.bitwise_and)
+        ts(v("cl"), v("Qa"), 0.0, A.is_equal)
+        mms([(v("P4", 0, 256), v("Q2"), v("cl"), False, True)])
+        mms([(v("P6", 0, 256), v("Y1"), v("cl"), True, True), (v("P6", 256, 512), v("Y2"), v("cl"), True, True)])
+        mms([(v("P5", 0, 256), v("Q1"), v("cl"), False, True)])
+        act(v("SF"), v("P6", 0, 512), F.Relu, 8192.0)
+        mms([(v("P2", 0, 256), v("Q1"), v("cl"), False, True)])
+        ts(v("H2c"), v("P4", 0, 256), 0.0, A.max, 2048.0, A.min)
+        lists("P7", 0, 16, "L", "H2c", 0, 256)
+        ts(v("F1c"), v("P5", 0, 256), -BIG, A.add, 0.0, A.max)
+        ts(v("F1u"), v("P2", 0, 256), -BIG, A.add, 0.0, A.max)
+        mms([(v("P3", 0, 256), v("blk"), v("F1c"), True, True)])
+        ts(v("gl"), v("P7", 0, 16), 2048.0, A.is_gt, 4095.0, A.mult)
+        ns, na, xs = "ns%d" % t, "na%d" % t, "xs%d" % t
+        tt(v(ns), v("gl"), v("P7", 0, 16), A.add)
+        dst = T.cores[(rank + h) % len(T.cores)]
+        rid, pid = topo.addr(dst, core)
+        es = topo.engines(core, dst)[:8]
+        mask = sum(1 << e for e in es)
+        src = T.cores[(rank - h) % len(T.cores)]
+        ein = len(topo.engines(src, core)[:8])
+
+        def send(buf, out, n, sem):
+            deps("G", True, [(buf, 0, n)], [])
+            g.remote_dma(out, T[buf][:], T.sem[sem], T.sem.loc, pid, rid, mask)
+            cnt["loc"] += len(es)
+            totals["loc"] = cnt["loc"]
+            totals[sem] = ein
+
+        send(ns, T[na][:], 16, "aN%d" % t)
+        lists("P5", 0, 16, "L", "F1c", 0, 256, True, False)
+        lists("P5", 0, 16, "L", "SF", 0, 256, False, True)
+        mms([(v("P0", 0, 32), v("Ib"), v("khi"), True, False), (v("P0", 0, 32), v("Ib"), v("klo"), False, False)] +
+            [(v("P0", 0, 32), m16("LK", r), v("SF", r, 512, 16), False, False) for r in range(16)] +
+            [(v("P0", 16, 32), m16("LK2", r), v("SF", r, 256, 16), False, r == 15) for r in range(16)])
+        copy(v("R1"), v("P3", 0, 256))
+        ts(v("c1L"), v("P5", 0, 16), -8192.0, A.add)
+        copy(v("zo16"), v("P0", 0, 32))
+        for q in range(16):
+            ts(v("EQ", 272 * q, 256 * q + 256), v("R1", 16 * q, 256), v("c1L", q, q + 1), A.is_equal)
+            if q == 0:
+                act(v("zz"), ind(v("Z"), v("zo16")), F.Copy)
+                mms([(v("P4", 0, 256), v("Ib"), v(("XW%d") % t, 0, 256), True, False), (v("P4", 0, 256), v("In"), v("zz", 256, 512), False, True)])
+                act(v(xs), v("P4", 0, 256), F.Abs)
+                lists("P7", 32, 16, "L0", "uh", 0, 256)
+                lists("P1", 0, 16, "L", "F1u", 0, 256, True, False)
+                lists("P1", 0, 16, "L", "SF", 0, 256, False, True)
+        send(xs, T[XW][:, 4096:4352], 256, "aX%d" % t)
+        mms([(v("P6", 0, 256), m16("Tq", 0), v("EQ", 0, 256), True, False)] +
+            [(v("P6", 16 * (q + 1), 256), v("blk"), v("EQ", 272 * q + 16, 256 * (q + 1)), False, False) for q in range(15)] +
+            [(v("P6", r, 256, 16), m16("Tq", r), v("EQ", r, 4096, 272), False, r == 15) for r in range(1, 16)])
+        act(v("cnr"), v("P6", 0, 256), F.Copy, -8192.0)
+        ts(v("cl16"), v("P5", 0, 16), -8193.0, A.add)
+        copy(v("c1h"), v("c1L"))
+        ts(v("si5"), v("si"), 5.0, A.mult)
+        tt(v("w1"), v("si5"), v("P7", 32, 48), A.add)
+        tt(v("nc"), ind(Sw, v("cl16")), v("F1u"), A.add)
+        ts(v("w2"), v("w1"), 2047, A.bitwise_and)
+        ts(v("nd"), v("nc"), 2047, A.bitwise_and)
+        ts(v("w3"), v("w2"), 2049.0, A.add)
+        tt(v("b0"), v("w3"), v("P5", 0, 16), A.max)
+        ts(v("b1"), v("b0"), -1.0, A.add)
+        mms([(v("P3", 0, 16), v("Ib"), v("c1h"), True, False)] +
+            [(v("P3", 0, 16), m16("Ea", r), v("cnr", r, 256, 16), False, r == 15) for r in range(16)])
+        if not last:
+            emit("V", [lambda: g.vector.tensor_reduce(out=T.gs[:], in_=T.gl[:], axis=AxisListType.X, op=A.add)], [("gl", 0, 16)], [("gs", 0, 1)])
+            mms([(v("P7", 64, 65), v("mones"), v("gs"), True, True)])
+        tt(v("so"), v("ip"), v("P3", 0, 16), A.max)
+        ts(v("so16"), v("so"), 255.0, A.add)
+        copy(ind(v("S"), v("so16")), v("nd"))
+        rec[na] = [(0, 16, ("aN%d" % t, ein, "R", {}), "w")]
+        tt(v("vi"), v("b1"), v(na), A.max)
+        ts(v("si"), v("vi"), 2047, A.bitwise_and)
+        copy(v("sl16"), v("si"))
+
+        def write_x(t=t, last=last):
+            copy(v("ux"), v("P1", 0, 16))
+            if not last:
+                copy(v("Ai"), v("P7", 64, 65))
+            ts(v("uy"), v("ux"), 8195, A.bitwise_and)
+            if not last:
+                ts(v("Aj"), v("Ai"), 15, A.bitwise_and)
+            tt(v("xo"), v("uy"), v("i4"), A.add)
+            if not last:
+                copy(v("Af"), v("Aj"))
+            copy(v("xo16"), v("xo"))
+            copy(ind(v("X", 0, XB0 + V), v("xo16")), v("zz", 0, 256))
+            if not last:
+                copy(ind(v("X", V, XB0 + 2 * V), v("xo16")), v("zz", 0, 256))
+
+        def half(t=t):
+            mms([(v("P7", 0, 256), v("Ih"), v("XW%d" % t, 0, 256), True, False), (v("P7", 0, 256), v("Ih"), v("zz", 0, 256), False, False),
+                 (v("P7", 0, 256), row("onesb", 128), row("cQ", 256), False, True)])
+            ts(v("XW%d" % t, 8192, 8448), v("P7", 0, 256), MAGIC, A.add, MAGIC, A.subtract)
+
+        def selx(t=t):
+            ts(v("sx"), v("vi"), 12288, A.bitwise_and)
+            tt(v("sy"), v("sx"), v("il"), A.add)
+            copy(v("sel16"), v("sy"))
+
+        def newx(t=t, last=last, ein=ein):
+            rec["XW%d" % t] = rec["XW%d" % t] + [(4096, 4352, ("aX%d" % t, ein, "R", {}), "w")]
+            act(v("XF") if last else v("XW%d" % (t + 1), 0, 256), ind(v("XW%d" % t), v("sel16")), F.Copy)
+
+        if not last:
+            later_v = [write_x, half, selx]
+            later_s = [newx]
+        else:
+            copy(v("yso"), v("si"))
+            dma("Y", T.ys[:], T.yso[:], [("yso", 0, 16)], [])
+            write_x()
+            dma("Y", T.yv[:], T.X[:, XB0:XB0 + V], [("X", XB0, XB0 + V)], [])
+            half()
+            selx()
+            newx()
+            dma("S", T.yx[:], T.XF[:], [("XF", 0, 256)], [])
+            for j in range(2):
+                copy(v("G", 1024 * j, 1024 * j + 1024), v("S", DUMP + 1024 * j, DUMP + 1024 * j + 1024))
+                mms([(v("P0", 0, 256), v("Ib"), v("G", 1024 * j + 256 * q, 1024 * j + 256 * q + 256), j == 0 and q == 0, j == 1 and q == 3) for q in range(4)])
+            act(v("yto"), v("P0", 0, 256), F.Copy)
+            dma("Y", T.yt[:], T.yto[:], [("yto", 0, 256)], [])
+    for s, n in totals.items():
+        g.sync.wait_ge(T.sem[s], n)

@@ -2,6 +2,9 @@ from concourse.mybir import AluOpType as A, AxisListType, ActivationFunctionType
 
 STEPS, W, V, I = 4, 2048, 1024, 256
 CHUNKS = [64, 64, 64, 64]
+SONLY, SPOS = False, 1
+Q0 = 9
+EW = 16 * (16 - Q0)
 DUMP = 256
 XB0 = 8192
 BIG = 4096.0
@@ -27,9 +30,8 @@ SCRATCH = {
     "Qi": ("sbuf", [128, 256], "int32"),
     "Qa": ("sbuf", [128, 256], "int32"),
     "cl": ("sbuf", [128, 256], "float16"),
-    "H2c": ("sbuf", [128, 256], "float16"),
-    "F1c": ("sbuf", [128, 256], "float16"),
-    "F1u": ("sbuf", [128, 256], "float16"),
+    "FH": ("sbuf", [128, 1024], "float16"),
+    "hs": ("sbuf", [128, 16], "float32"),
     "SF": ("sbuf", [128, 512], "bfloat16"),
     "R1": ("sbuf", [128, 256], "float16"),
     "cnr": ("sbuf", [128, 256], "bfloat16"),
@@ -38,25 +40,27 @@ SCRATCH = {
     "nd": ("sbuf", [128, 256], "int32"),
     "XF": ("sbuf", [128, 256], "bfloat16"),
     "yto": ("sbuf", [128, 256], "float32"),
-    "c1L": ("sbuf", [128, 16], "float32"), "cl16": ("sbuf", [128, 16], "uint16"), "zo16": ("sbuf", [128, 32], "uint16"),
-    "gl": ("sbuf", [128, 16], "float32"), "gs": ("sbuf", [128, 1], "float32"), "Ai": ("sbuf", [128, 1], "int32"),
-    "Aj": ("sbuf", [128, 1], "int32"), "Af": ("sbuf", [128, 1], "float32"),
+    "c1L": ("sbuf", [128, 16], "float32"), "c1P": ("sbuf", [128, 16], "float32"), "cl16": ("sbuf", [128, 16], "uint16"), "zo16": ("sbuf", [128, 32], "uint16"),
+    "gl": ("sbuf", [128, 16], "float32"), "gs": ("sbuf", [128, 1], "float32"),
     "ux": ("sbuf", [128, 16], "int32"), "uy": ("sbuf", [128, 16], "int32"), "xo": ("sbuf", [128, 16], "float32"),
     "xo16": ("sbuf", [128, 16], "uint16"), "so": ("sbuf", [128, 16], "float32"), "so16": ("sbuf", [128, 16], "uint16"),
-    "si5": ("sbuf", [128, 16], "float32"), "w1": ("sbuf", [128, 16], "int32"), "w2": ("sbuf", [128, 16], "int32"),
-    "w3": ("sbuf", [128, 16], "float32"), "b0": ("sbuf", [128, 16], "float32"), "b1": ("sbuf", [128, 16], "float32"),
+    "w1": ("sbuf", [128, 16], "int32"), "w2": ("sbuf", [128, 16], "int32"),
+    "w3": ("sbuf", [128, 16], "float32"), "b0": ("sbuf", [128, 16], "float32"),
     "vi": ("sbuf", [128, 16], "int32"), "si": ("sbuf", [128, 16], "int32"), "sl16": ("sbuf", [128, 16], "uint16"),
     "sx": ("sbuf", [128, 16], "int32"), "sy": ("sbuf", [128, 16], "float32"), "sel16": ("sbuf", [128, 16], "uint16"),
     "sA": ("sbuf", [128, 16], "float16"), "yso": ("sbuf", [128, 16], "float32"),
-    "onesb": ("sbuf", [128, 128], "bfloat16"), "mones": ("sbuf", [128, 128], "float32"),
+    "onesb": ("sbuf", [128, 128], "bfloat16"),
     "Ib": ("sbuf", [128, 128], "bfloat16"), "Jb": ("sbuf", [128, 128], "bfloat16"), "blk": ("sbuf", [128, 128], "bfloat16"),
     "tr": ("sbuf", [128, 128], "bfloat16"), "Y1": ("sbuf", [128, 128], "bfloat16"), "Y2": ("sbuf", [128, 128], "bfloat16"),
     "Q1": ("sbuf", [128, 128], "bfloat16"), "Q2": ("sbuf", [128, 128], "bfloat16"), "I32": ("sbuf", [128, 128], "bfloat16"),
-    "L0": ("sbuf", [128, 2048], "bfloat16"), "cF": ("sbuf", [128, 256], "float16"), "c1h": ("sbuf", [128, 16], "float16"), "Ih": ("sbuf", [128, 128], "bfloat16"), "In": ("sbuf", [128, 128], "bfloat16"),
+    "cF": ("sbuf", [128, 256], "float16"), "c1h": ("sbuf", [128, 16], "float16"), "Ih": ("sbuf", [128, 128], "bfloat16"), "In": ("sbuf", [128, 128], "bfloat16"),
     "Ea": ("sbuf", [128, 2048], "bfloat16"), "Eb": ("sbuf", [128, 2048], "bfloat16"), "Wm": ("sbuf", [128, 2048], "bfloat16"),
     "L": ("sbuf", [128, 2048], "bfloat16"), "LK": ("sbuf", [128, 2048], "bfloat16"), "LK2": ("sbuf", [128, 2048], "bfloat16"),
     "Lp": ("sbuf", [128, 2048], "bfloat16"), "Tr": ("sbuf", [128, 2048], "bfloat16"), "Lq": ("sbuf", [128, 2048], "bfloat16"),
     "Tq": ("sbuf", [128, 2048], "bfloat16"),
+    "EA": ("sbuf", [128, EW * (16 - Q0)], "bfloat16"), "EB": ("sbuf", [128, EW * (16 - Q0)], "bfloat16"),
+    "nb": ("sbuf", [128, 16], "float32"), "gf": ("sbuf", [128, 16], "float32"),
+    "gB": ("sbuf", [128, 128], "bfloat16"), "c32": ("sbuf", [128, 256], "bfloat16"), "I5": ("sbuf", [128, 128], "bfloat16"),
     "cB": ("sbuf", [128, 256], "bfloat16"), "cQ": ("sbuf", [128, 256], "bfloat16"),
     "khi": ("sbuf", [128, 32], "bfloat16"), "klo": ("sbuf", [128, 32], "bfloat16"),
     "pi": ("sbuf", [128, 1], "int32"), "pa": ("sbuf", [128, 1], "int32"), "pg": ("sbuf", [128, 1], "int32"),
@@ -187,10 +191,12 @@ def rank_program(g, core, T, topo):
 
     def act(out, in_, f, scale=1.0, bias=0.0):
         rd = split(in_)
-        sc = scale
+        sc, bi = scale, bias
         if isinstance(scale, tuple):
             rd = rd + scale[1]; sc = scale[0]
-        emit("S", [lambda: g.scalar.activation(out=out[0], in_=in_[0], func=f, bias=bias, scale=sc)], rd, out[1])
+        if isinstance(bias, tuple):
+            rd = rd + bias[1]; bi = bias[0]
+        emit("S", [lambda: g.scalar.activation(out=out[0], in_=in_[0], func=f, bias=bi, scale=sc)], rd, out[1])
 
     def mms(items):
         calls, rd, wr = [], [], []
@@ -203,25 +209,22 @@ def rank_program(g, core, T, topo):
     def iota(out, pattern, base, cm, flag=True):
         emit("G", [lambda: g.iota(out[0], pattern, base, cm, allow_small_or_imprecise_dtypes=flag)], [], out[1])
 
-    def asel(out, in_, pattern, op, base, cm):
-        emit("G", [lambda: g.affine_select(out[0], in_[0], pattern, op, 0.0, base, cm)], in_[1], out[1])
+    def asel(out, in_, pattern, op, base, cm, other=0.0):
+        emit("G", [lambda: g.affine_select(out[0], in_[0], pattern, op, other, base, cm)], in_[1], out[1])
 
     def m16(n, r):
         return v(n, 128 * r, 128 * r + 128)
 
     dma("Y", T.si[:], T.s0[:], [], [("si", 0, 16)])
     dma("S", T.S[:, DUMP + 1024:DUMP + 2048], T.stm[:, 1024:2048], [], [("S", DUMP + 1024, DUMP + 2048)])
-    dma("Y", T.S[:, DUMP:DUMP + 1024], T.stm[:, 0:1024], [], [("S", DUMP, DUMP + 1024)])
     dma("Y", T.wi[:], T.wt[:], [], [("wi", 0, 1)])
+    dma("Y", T.S[:, DUMP:DUMP + 1024], T.stm[:, 0:1024], [], [("S", DUMP, DUMP + 1024)])
     dma("Y", T.X[:, XB0:XB0 + V], T.vx[:], [], [("X", XB0, XB0 + V)])
     dma("Y", T.X[:, XB0 + V:XB0 + 2 * V], T.vx[:], [], [("X", XB0 + V, XB0 + 2 * V)])
     dma("Y", T.XW0[:, 0:256], T.x0[:], [], [("XW0", 0, 256)])
 
     iota(v("pi"), [[0, 1]], 0, 1, False)
     fill(v("onesb"), 1.0)
-    fill(v("L"), 0.0)
-    fill(v("cB"), -BIG)
-    fill(v("Lq"), -32.0)
     iota(v("cg"), [[1, 8], [0, 16]], 0, 0)
     iota(v("kk"), [[1, 16]], 0, 0)
     asel(v("Ib"), v("onesb"), [[-1, 128]], A.is_equal, 0, 1)
@@ -232,20 +235,23 @@ def rank_program(g, core, T, topo):
     copy(v("pgf"), v("pg"))
     ts(v("blk"), v("cg"), v("pgf"), A.is_equal)
     ts(v("K16"), v("kk"), v("p15"), A.is_equal)
-    copy(v("sl16"), v("si"))
+    for k in range(16):
+        act(m16("Eb", k), v("Jb"), F.Copy, v("K16", k ^ 1, (k ^ 1) + 1))
+    fill(v("Lq"), 0.0)
+    fill(v("cB"), -BIG)
     for k in range(16):
         ts(m16("Ea", k), v("Ib"), v("K16", k, k + 1), A.mult)
-        ts(m16("Eb", k), v("Jb"), v("K16", k ^ 1, (k ^ 1) + 1), A.mult)
-    for r in range(16):
-        act(v("L", 128 * r + r, 128 * r + 128, 16), v("blk", r, 128, 16), F.Copy)
+    fill(v("L"), 0.0)
+    copy(v("sl16"), v("si"))
+    copy(v("wf"), v("wi"))
+    asel(v("tr"), v("blk"), [[1, 128]], A.is_gt, 0, -1)
     iota(v("i16"), [[16, 16]], 0, 0)
     iota(v("khi"), [[0, 2], [256, 16]], 0, 0)
-    asel(v("tr"), v("blk"), [[1, 128]], A.is_gt, 0, -1)
-    asel(v("Lp"), v("Lq"), [[-1, 16], [-16, 8], [0, 16]], A.is_equal, 0, 1)
-    fill(v("Tq"), 1.0)
-    asel(v("Tr"), v("Tq"), [[1, 16], [16, 8], [0, 16]], A.is_ge, -1, -1)
+    asel(v("Lp"), v("Lq"), [[-1, 16], [-16, 8], [0, 16]], A.not_equal, 0, 1, -32.0)
+    asel(v("Tr"), v("Lq"), [[-1, 16], [-16, 8], [0, 16]], A.is_ge, 0, 1, 1.0)
     asel(v("Tq"), v("Tr"), [[0, 16], [-16, 8], [0, 16]], A.is_ge, 0, 1)
-    copy(v("wf"), v("wi"))
+    for r in range(16):
+        act(v("L", 128 * r + r, 128 * r + 128, 16), v("blk", r, 128, 16), F.Copy)
     act(v("Wm"), v("L"), F.Copy, v("wf"))
     ts(v("k0"), v("p15"), 0.0, A.is_equal)
     ts(v("kc"), v("p15"), 1.0, A.add, 1.0 / 8192, A.mult)
@@ -255,20 +261,19 @@ def rank_program(g, core, T, topo):
     ts(v("i4"), v("il"), 4.0, A.mult)
     ts(v("ip"), v("il"), -255.0, A.add)
     ts(v("cF"), v("cB"), 0.0, A.mult, -HALF, A.add)
-    act(v("L0"), v("L"), F.Copy, v("k0"))
     ts(v("klo"), v("khi"), 0.0, A.mult, v("kl"), A.add)
     tt(v("Y1"), v("Ib"), v("tr"), A.subtract)
     tt(v("Y2"), v("Y1"), v("Ib"), A.add)
-    fill(v("Af"), 0.0)
-    fill(v("mones"), -1.0)
     fill(v("cQ"), -0.25)
+    fill(v("c32"), 32.0)
+    act(v("I5"), v("Ib"), F.Copy, 5.0)
     act(v("I32"), v("Ib"), F.Copy, 32.0)
     act(v("Ih"), v("Ib"), F.Copy, 0.5)
     act(v("In"), v("Ib"), F.Copy, -1.0)
     act(v("Q1"), v("Y1"), F.Copy, BIG)
     act(v("Q2"), v("Y2"), F.Copy, BIG)
     act(v("LK"), v("L"), F.Copy, v("kc"))
-    act(v("LK2"), v("L"), F.Copy, v("kc2"))
+    ts(v("LK2"), v("L"), v("kc2"), A.mult)
 
     Sw = v("S", DUMP, DUMP + W)
     Xw = v("X", XB0, XB0 + 2 * V)
@@ -298,41 +303,77 @@ def rank_program(g, core, T, topo):
         def conv(j):
             i0, i1 = starts[j], starts[j + 1]
             copy(v("lab", 2 * i0, 2 * i1), v("P%d" % (j % 2), 0, 2 * (i1 - i0)))
+
+        def load_b(j):
+            i0, i1 = starts[j], starts[j + 1]
             act(v("XB", 16 * i0, 16 * i1), ind(Xw, v("lab", i0 + i1, 2 * i1)), F.Copy)
+
+        def load_a(j):
+            i0, i1 = starts[j], starts[j + 1]
+            act(v("D", 16 * i0, 16 * i1), ind(Xw, v("lab", 2 * i0, i0 + i1)), F.Copy)
+            for q in range(16 * i0, 16 * i1, 512):
+                e = min(q + 512, 16 * i1)
+                b = ("P6", "P7")[(q - 16 * i0) // 512 % 2]
+                mms([(v(b, 0, e - q), v("Ib"), v("D", q, e), True, False), (v(b, 0, e - q), v("In"), v("XB", q, e), False, True)])
+
+        def size_p(j):
+            i0, i1 = starts[j], starts[j + 1]
+            for q in range(16 * i0, 16 * i1, 512):
+                e = min(q + 512, 16 * i1)
+                act(v("Z", q, e), v(("P6", "P7")[(q - 16 * i0) // 512 % 2], 0, e - q), F.Abs)
+
+        def size(j):
+            i0, i1 = starts[j], starts[j + 1]
+            act(v("Z", 16 * i0, 16 * i1), v("D", 16 * i0, 16 * i1), F.Abs)
+
+        def weigh(j, fin=False):
+            i0, i1 = starts[j], starts[j + 1]
+            mms([(v("P2", i0, i1), m16("Wm", k), v("Z", 16 * i0 + k, 16 * i1, 16), False, fin and k == 15) for k in range(16)])
 
         def diff(j):
             i0, i1 = starts[j], starts[j + 1]
             tt(v("D", 16 * i0, 16 * i1), ind(Xw, v("lab", 2 * i0, i0 + i1)), v("XB", 16 * i0, 16 * i1), A.subtract)
-            act(v("Z", 16 * i0, 16 * i1), v("D", 16 * i0, 16 * i1), F.Abs)
-            mms([(v("P2", i0, i1), m16("Wm", k), v("Z", 16 * i0 + k, 16 * i1, 16), False, k == 15 and i1 == I) for k in range(16)])
 
         gath(0)
         sel(0)
-        ts(v("c16p"), v("c16"), 1.0, A.add)
-        for f in later_v:
-            f()
-        ts(v("sA"), v("si"), v("Af"), A.subtract, 7.0, A.subtract)
-        gath(1)
-        sel(1)
-        conv(0)
-        for f in later_s:
-            f()
-        gath(2)
-        sel(2)
-        conv(1)
-        mms([(v("P2", 0, 256), row("onesb", 128), row("cF", 256), True, False)])
-        mms([(v("P3", 0, 256), v("I32"), v("c16p"), True, False)] +
-            [(v("P3", r, 256, 16), m16("Lp", r), v("sA"), False, r == 15) for r in range(16)])
-        mms([(v("P4", 0, 256), v("Ib"), v("c16p"), True, False), (v("P4", 0, 256), row("onesb", 128), row("cB", 256), False, False)])
-        mms([(v("P5", 0, 256), v("Ib"), v("c16p"), True, False)])
-        gath(3)
-        sel(3)
-        conv(2)
+        if later_v:
+            later_v[0]()
+        else:
+            ts(v("c16p"), v("c16"), 1.0, A.add)
+            ts(v("sA"), v("si"), 7.0, A.subtract)
+        n = len(CHUNKS)
+        for j in range(1, n):
+            gath(j)
+            sel(j)
+            conv(j - 1)
+            load_b(j - 1)
+            if j == 1:
+                for f in later_v[1:]:
+                    f()
+            if j == 2:
+                for f in later_s:
+                    f()
+                mms([(v("P2", 0, 256), row("onesb", 128), row("cF", 256), True, False)])
+                mms([(v("P3", 0, 256), v("I32"), v("c16p"), True, False)] +
+                    ([(v("P3", 0, 256), v("gB"), v("c32"), False, False)] if t else []) +
+                    [(v("P3", r, 256, 16), m16("Lp", r), v("sA"), False, r == 15) for r in range(16)])
+                mms([(v("P4", 0, 256), v("Ib"), v("c16p"), True, False), (v("P4", 0, 256), row("onesb", 128), row("cB", 256), False, False)])
+                mms([(v("P5", 0, 256), v("Ib"), v("c16p"), True, False)])
         diff(0)
-        conv(3)
-        diff(1)
-        diff(2)
-        diff(3)
+        conv(n - 1)
+        load_b(n - 1)
+        m = n
+        if SONLY:
+            m = n - 1
+            load_a(m)
+        for j in range(m):
+            if j + 1 < m:
+                diff(j + 1)
+            size(j)
+            weigh(j, j == m - 1)
+            if j == SPOS and SONLY:
+                size_p(m)
+                weigh(m)
         ts(v("N1"), v("P2", 0, 256), M2K, A.add, M2K, A.subtract)
         tt(v("uq"), v("P2", 0, 256), v("N1"), A.subtract)
         act(v("sq"), v("uq"), F.Square, 1.0, HALF + 16.0)
@@ -341,19 +382,25 @@ def rank_program(g, core, T, topo):
         tt(v("Qi"), v("sq"), v("P3", 0, 256), A.add)
         ts(v("Qa"), v("Qi"), 480, A.bitwise_and)
         ts(v("cl"), v("Qa"), 0.0, A.is_equal)
+        mms([(v("P5", 0, 256), v("Q1"), v("cl"), False, True)])
         mms([(v("P4", 0, 256), v("Q2"), v("cl"), False, True)])
         mms([(v("P6", 0, 256), v("Y1"), v("cl"), True, True), (v("P6", 256, 512), v("Y2"), v("cl"), True, True)])
-        mms([(v("P5", 0, 256), v("Q1"), v("cl"), False, True)])
         act(v("SF"), v("P6", 0, 512), F.Relu, 8192.0)
         mms([(v("P2", 0, 256), v("Q1"), v("cl"), False, True)])
-        ts(v("H2c"), v("P4", 0, 256), 0.0, A.max, 2048.0, A.min)
-        lists("P7", 0, 16, "L", "H2c", 0, 256)
-        ts(v("F1c"), v("P5", 0, 256), -BIG, A.add, 0.0, A.max)
-        ts(v("F1u"), v("P2", 0, 256), -BIG, A.add, 0.0, A.max)
-        mms([(v("P3", 0, 256), v("blk"), v("F1c"), True, True)])
-        ts(v("gl"), v("P7", 0, 16), 2048.0, A.is_gt, 4095.0, A.mult)
+        ts(v("FH", 768, 1024), v("uq"), HALF, A.add, v("k0"), A.mult)
+        ts(v("FH", 0, 256), v("P5", 0, 256), -BIG, A.add, 0.0, A.max)
+        mms([(v("P3", 0, 256), v("blk"), v("FH", 0, 256), True, True)])
+        ts(v("FH", 256, 512), v("P4", 0, 256), 0.0, A.max, 2048.0, A.min)
+        lists("P7", 0, 32, "L", "FH", 0, 512)
+        copy(v("R1"), v("P3", 0, 256))
+        ts(v("FH", 512, 768), v("P2", 0, 256), -BIG, A.add, 0.0, A.max)
+        lists("P5", 0, 32, "L", "FH", 512, 1024, True, False)
+        mms([(v("P5", 16, 32), v("I5"), v("sA"), False, True)])
+        ts(v("c1L"), v("P7", 0, 16), -1.0, A.add)
+        ts(v("gl"), v("P7", 16, 32), 2048.0, A.is_gt, 4095.0, A.mult)
         ns, na, xs = "ns%d" % t, "na%d" % t, "xs%d" % t
-        tt(v(ns), v("gl"), v("P7", 0, 16), A.add)
+        tt(v(ns), v("gl"), v("P7", 16, 32), A.add)
+        act(v("nb"), v("P7", 0, 16), F.Copy, -1.0)
         dst = T.cores[(rank + h) % len(T.cores)]
         rid, pid = topo.addr(dst, core)
         es = topo.engines(core, dst)[:8]
@@ -369,70 +416,70 @@ def rank_program(g, core, T, topo):
             totals[sem] = ein
 
         send(ns, T[na][:], 16, "aN%d" % t)
-        lists("P5", 0, 16, "L", "F1c", 0, 256, True, False)
-        lists("P5", 0, 16, "L", "SF", 0, 256, False, True)
         mms([(v("P0", 0, 32), v("Ib"), v("khi"), True, False), (v("P0", 0, 32), v("Ib"), v("klo"), False, False)] +
             [(v("P0", 0, 32), m16("LK", r), v("SF", r, 512, 16), False, False) for r in range(16)] +
             [(v("P0", 16, 32), m16("LK2", r), v("SF", r, 256, 16), False, r == 15) for r in range(16)])
-        copy(v("R1"), v("P3", 0, 256))
-        ts(v("c1L"), v("P5", 0, 16), -8192.0, A.add)
+        for q in range(Q0):
+            ts(v("EQ", 272 * q, 256 * q + 256), v("R1", 16 * q, 256), v("c1L", q, q + 1), A.subtract, 1.0, A.is_equal)
         copy(v("zo16"), v("P0", 0, 32))
-        for q in range(16):
-            ts(v("EQ", 272 * q, 256 * q + 256), v("R1", 16 * q, 256), v("c1L", q, q + 1), A.is_equal)
-            if q == 0:
-                act(v("zz"), ind(v("Z"), v("zo16")), F.Copy)
-                mms([(v("P4", 0, 256), v("Ib"), v(("XW%d") % t, 0, 256), True, False), (v("P4", 0, 256), v("In"), v("zz", 256, 512), False, True)])
-                act(v(xs), v("P4", 0, 256), F.Abs)
-                lists("P7", 32, 16, "L0", "uh", 0, 256)
-                lists("P1", 0, 16, "L", "F1u", 0, 256, True, False)
-                lists("P1", 0, 16, "L", "SF", 0, 256, False, True)
-        send(xs, T[XW][:, 4096:4352], 256, "aX%d" % t)
+        for q in range(Q0, 16):
+            n = EW * (q - Q0)
+            act(v("EA", n, n + EW), v("P3", 16 * Q0, 256), F.Abs, 1.0, v("nb", q, q + 1))
+        act(v("EB"), v("EA"), F.Relu, -1.0, 1.0)
+        act(v("zz"), ind(v("Z"), v("zo16")), F.Copy)
         mms([(v("P6", 0, 256), m16("Tq", 0), v("EQ", 0, 256), True, False)] +
-            [(v("P6", 16 * (q + 1), 256), v("blk"), v("EQ", 272 * q + 16, 256 * (q + 1)), False, False) for q in range(15)] +
-            [(v("P6", r, 256, 16), m16("Tq", r), v("EQ", r, 4096, 272), False, r == 15) for r in range(1, 16)])
+            [(v("P6", 16 * (q + 1), 256), v("blk"), v("EQ", 272 * q + 16, 256 * (q + 1)), False, False) for q in range(Q0)] +
+            [(v("P6", r, 16 * Q0, 16), m16("Tq", r), v("EQ", r, 272 * Q0 - 16, 272), False, False) for r in range(1, 16)])
+        mms([(v("P6", 16 * (q + 1), 256), v("blk"), v("EB", EW * (q - Q0) + 16 * (q - Q0 + 1), EW * (q - Q0 + 1)), False, False) for q in range(Q0, 15)] +
+            [(v("P6", 16 * Q0 + r, 256, 16), m16("Tq", r), v("EB", r, EW * (16 - Q0), EW + 16), False, r == 15) for r in range(1, 16)])
+        mms([(v("P4", 0, 256), v("Ib"), v(XW, 0, 256), True, False), (v("P4", 0, 256), v("In"), v("zz", 256, 512), False, True)])
+        mms([(v("P4", 256, 512), v("Ih"), v(XW, 0, 256), True, False), (v("P4", 256, 512), v("Ih"), v("zz", 0, 256), False, False),
+             (v("P4", 256, 512), row("onesb", 128), row("cQ", 256), False, True)])
         act(v("cnr"), v("P6", 0, 256), F.Copy, -8192.0)
-        ts(v("cl16"), v("P5", 0, 16), -8193.0, A.add)
-        copy(v("c1h"), v("c1L"))
-        ts(v("si5"), v("si"), 5.0, A.mult)
-        tt(v("w1"), v("si5"), v("P7", 32, 48), A.add)
-        tt(v("nc"), ind(Sw, v("cl16")), v("F1u"), A.add)
+        act(v(xs), v("P4", 0, 256), F.Abs)
+        act(v("N1"), v("P4", 256, 512), F.Identity, 1.0, MAGIC)
+        send(xs, T[XW][:, 4096:4352], 256, "aX%d" % t)
+        act(v(XW, 8192, 8448), v("N1"), F.Identity, 1.0, -MAGIC)
+        if not last:
+            emit("S", [lambda: g.scalar.activation(out=T.gf[:], in_=T.gl[:], func=F.Sign, accum_out=T.gs[:])], [("gl", 0, 16)], [("gf", 0, 16), ("gs", 0, 1)])
+            act(v("gB"), v("onesb"), F.Copy, v("gs"))
+        copy(v("cl16"), v("c1L"))
+        ts(v("hs"), v("c1L"), 0.0, A.is_ge, 8192.0, A.mult)
+        ts(v("w1"), v("P5", 16, 32), 35.0, A.add)
+        tt(v("c1P"), v("c1L"), v("hs"), A.add)
+        tt(v("ux"), v("hs"), v("P5", 0, 16), A.add)
+        ts(v("c1h"), v("c1P"), -8191.0, A.add)
+        tt(v("nc"), ind(Sw, v("cl16")), v("FH", 512, 768), A.add)
         ts(v("w2"), v("w1"), 2047, A.bitwise_and)
         ts(v("nd"), v("nc"), 2047, A.bitwise_and)
-        ts(v("w3"), v("w2"), 2049.0, A.add)
-        tt(v("b0"), v("w3"), v("P5", 0, 16), A.max)
-        ts(v("b1"), v("b0"), -1.0, A.add)
+        ts(v("w3"), v("w2"), 2048.0, A.add)
+        tt(v("b0"), v("w3"), v("c1P"), A.max)
         mms([(v("P3", 0, 16), v("Ib"), v("c1h"), True, False)] +
             [(v("P3", 0, 16), m16("Ea", r), v("cnr", r, 256, 16), False, r == 15) for r in range(16)])
-        if not last:
-            emit("V", [lambda: g.vector.tensor_reduce(out=T.gs[:], in_=T.gl[:], axis=AxisListType.X, op=A.add)], [("gl", 0, 16)], [("gs", 0, 1)])
-            mms([(v("P7", 64, 65), v("mones"), v("gs"), True, True)])
+        ts(v("uy"), v("ux"), 8195, A.bitwise_and)
+        tt(v("xo"), v("uy"), v("i4"), A.add)
+        copy(v("xo16"), v("xo"))
+        copy(ind(v("X", 0, XB0 + V), v("xo16")), v("zz", 0, 256))
         tt(v("so"), v("ip"), v("P3", 0, 16), A.max)
         ts(v("so16"), v("so"), 255.0, A.add)
         copy(ind(v("S"), v("so16")), v("nd"))
+
+        def write_x():
+            ts(v("c16p"), v("c16"), 1.0, A.add)
+            ts(v("sA"), v("si"), 7.0, A.subtract)
+            copy(ind(v("X", V, XB0 + 2 * V), v("xo16")), v("zz", 0, 256))
+
+        if last:
+            for j in range(2):
+                copy(v("G", 1024 * j, 1024 * j + 1024), v("S", DUMP + 1024 * j, DUMP + 1024 * j + 1024))
+                mms([(v("P0", 0, 256), v("Ib"), v("G", 1024 * j + 256 * q, 1024 * j + 256 * q + 256), j == 0 and q == 0, j == 1 and q == 3) for q in range(4)])
+            act(v("yto"), v("P0", 0, 256), F.Copy)
+            dma("Y", T.yv[:], T.X[:, XB0:XB0 + V], [("X", XB0, XB0 + V)], [])
+            dma("Y", T.yt[:], T.yto[:], [("yto", 0, 256)], [])
         rec[na] = [(0, 16, ("aN%d" % t, ein, "R", {}), "w")]
-        tt(v("vi"), v("b1"), v(na), A.max)
+        tt(v("vi"), v("b0"), v(na), A.max)
         ts(v("si"), v("vi"), 2047, A.bitwise_and)
         copy(v("sl16"), v("si"))
-
-        def write_x(t=t, last=last):
-            copy(v("ux"), v("P1", 0, 16))
-            if not last:
-                copy(v("Ai"), v("P7", 64, 65))
-            ts(v("uy"), v("ux"), 8195, A.bitwise_and)
-            if not last:
-                ts(v("Aj"), v("Ai"), 15, A.bitwise_and)
-            tt(v("xo"), v("uy"), v("i4"), A.add)
-            if not last:
-                copy(v("Af"), v("Aj"))
-            copy(v("xo16"), v("xo"))
-            copy(ind(v("X", 0, XB0 + V), v("xo16")), v("zz", 0, 256))
-            if not last:
-                copy(ind(v("X", V, XB0 + 2 * V), v("xo16")), v("zz", 0, 256))
-
-        def half(t=t):
-            mms([(v("P7", 0, 256), v("Ih"), v("XW%d" % t, 0, 256), True, False), (v("P7", 0, 256), v("Ih"), v("zz", 0, 256), False, False),
-                 (v("P7", 0, 256), row("onesb", 128), row("cQ", 256), False, True)])
-            ts(v("XW%d" % t, 8192, 8448), v("P7", 0, 256), MAGIC, A.add, MAGIC, A.subtract)
 
         def selx(t=t):
             ts(v("sx"), v("vi"), 12288, A.bitwise_and)
@@ -444,21 +491,13 @@ def rank_program(g, core, T, topo):
             act(v("XF") if last else v("XW%d" % (t + 1), 0, 256), ind(v("XW%d" % t), v("sel16")), F.Copy)
 
         if not last:
-            later_v = [write_x, half, selx]
+            later_v = [write_x, selx]
             later_s = [newx]
         else:
             copy(v("yso"), v("si"))
             dma("Y", T.ys[:], T.yso[:], [("yso", 0, 16)], [])
-            write_x()
-            dma("Y", T.yv[:], T.X[:, XB0:XB0 + V], [("X", XB0, XB0 + V)], [])
-            half()
             selx()
             newx()
             dma("S", T.yx[:], T.XF[:], [("XF", 0, 256)], [])
-            for j in range(2):
-                copy(v("G", 1024 * j, 1024 * j + 1024), v("S", DUMP + 1024 * j, DUMP + 1024 * j + 1024))
-                mms([(v("P0", 0, 256), v("Ib"), v("G", 1024 * j + 256 * q, 1024 * j + 256 * q + 256), j == 0 and q == 0, j == 1 and q == 3) for q in range(4)])
-            act(v("yto"), v("P0", 0, 256), F.Copy)
-            dma("Y", T.yt[:], T.yto[:], [("yto", 0, 256)], [])
     for s, n in totals.items():
         g.sync.wait_ge(T.sem[s], n)

from concourse.mybir import AluOpType as A, AxisListType, ActivationFunctionType as F

STEPS, W, V, I = 4, 2048, 1024, 256
CHUNKS = [64, 64, 64, 64]
SONLY, SPOS = False, 1
Q0 = 9
EW = 16 * (16 - Q0)
DUMP = 256
XB0 = 8192
BIG = 4096.0
HALF = 1023.5
M2K = 25769803776.0
MAGIC = 12582912.0

SCRATCH = {
    "S": ("sbuf", [128, DUMP + W], "int32"),
    "X": ("sbuf", [128, XB0 + 2 * V], "bfloat16"),
    "G": ("sbuf", [128, 4096], "float16"),
    "XB": ("sbuf", [128, 4096], "bfloat16"),
    "D": ("sbuf", [128, 4096], "bfloat16"),
    "Z": ("sbuf", [128, 4096], "bfloat16"),
    "EQ": ("sbuf", [128, 4096], "float16"),
    "c16": ("sbuf", [128, 256], "uint16"),
    "lab": ("sbuf", [128, 512], "uint16"),
    "c16p": ("sbuf", [128, 256], "float16"),
    "sq": ("sbuf", [128, 256], "float32"),
    "N1": ("sbuf", [128, 256], "float32"),
    "uq": ("sbuf", [128, 256], "float32"),
    "uh": ("sbuf", [128, 256], "float16"),
    "Qi": ("sbuf", [128, 256], "int32"),
    "Qa": ("sbuf", [128, 256], "int32"),
    "cl": ("sbuf", [128, 256], "float16"),
    "FH": ("sbuf", [128, 1024], "float16"),
    "hs": ("sbuf", [128, 16], "float32"),
    "SF": ("sbuf", [128, 512], "bfloat16"),
    "R1": ("sbuf", [128, 256], "float16"),
    "cnr": ("sbuf", [128, 256], "bfloat16"),
    "zz": ("sbuf", [128, 512], "bfloat16"),
    "nc": ("sbuf", [128, 256], "int32"),
    "nd": ("sbuf", [128, 256], "int32"),
    "XF": ("sbuf", [128, 256], "bfloat16"),
    "yto": ("sbuf", [128, 256], "float32"),
    "c1L": ("sbuf", [128, 16], "float32"), "c1P": ("sbuf", [128, 16], "float32"), "cl16": ("sbuf", [128, 16], "uint16"), "zo16": ("sbuf", [128, 32], "uint16"),
    "gl": ("sbuf", [128, 16], "float32"), "gs": ("sbuf", [128, 1], "float32"),
    "ux": ("sbuf", [128, 16], "int32"), "uy": ("sbuf", [128, 16], "int32"), "xo": ("sbuf", [128, 16], "float32"),
    "xo16": ("sbuf", [128, 16], "uint16"), "so": ("sbuf", [128, 16], "float32"), "so16": ("sbuf", [128, 16], "uint16"),
    "w1": ("sbuf", [128, 16], "int32"), "w2": ("sbuf", [128, 16], "int32"),
    "w3": ("sbuf", [128, 16], "float32"), "b0": ("sbuf", [128, 16], "float32"),
    "vi": ("sbuf", [128, 16], "int32"), "si": ("sbuf", [128, 16], "int32"), "sl16": ("sbuf", [128, 16], "uint16"),
    "sx": ("sbuf", [128, 16], "int32"), "sy": ("sbuf", [128, 16], "float32"), "sel16": ("sbuf", [128, 16], "uint16"),
    "sA": ("sbuf", [128, 16], "float16"), "yso": ("sbuf", [128, 16], "float32"),
    "onesb": ("sbuf", [128, 128], "bfloat16"),
    "Ib": ("sbuf", [128, 128], "bfloat16"), "Jb": ("sbuf", [128, 128], "bfloat16"), "blk": ("sbuf", [128, 128], "bfloat16"),
    "tr": ("sbuf", [128, 128], "bfloat16"), "Y1": ("sbuf", [128, 128], "bfloat16"), "Y2": ("sbuf", [128, 128], "bfloat16"),
    "Q1": ("sbuf", [128, 128], "bfloat16"), "Q2": ("sbuf", [128, 128], "bfloat16"), "I32": ("sbuf", [128, 128], "bfloat16"),
    "cF": ("sbuf", [128, 256], "float16"), "c1h": ("sbuf", [128, 16], "float16"), "Ih": ("sbuf", [128, 128], "bfloat16"), "In": ("sbuf", [128, 128], "bfloat16"),
    "Ea": ("sbuf", [128, 2048], "bfloat16"), "Eb": ("sbuf", [128, 2048], "bfloat16"), "Wm": ("sbuf", [128, 2048], "bfloat16"),
    "L": ("sbuf", [128, 2048], "bfloat16"), "LK": ("sbuf", [128, 2048], "bfloat16"), "LK2": ("sbuf", [128, 2048], "bfloat16"),
    "Lp": ("sbuf", [128, 2048], "bfloat16"), "Tr": ("sbuf", [128, 2048], "bfloat16"), "Lq": ("sbuf", [128, 2048], "bfloat16"),
    "Tq": ("sbuf", [128, 2048], "bfloat16"),
    "EA": ("sbuf", [128, EW * (16 - Q0)], "bfloat16"), "EB": ("sbuf", [128, EW * (16 - Q0)], "bfloat16"),
    "nb": ("sbuf", [128, 16], "float32"), "gf": ("sbuf", [128, 16], "float32"),
    "gB": ("sbuf", [128, 128], "bfloat16"), "c32": ("sbuf", [128, 256], "bfloat16"), "I5": ("sbuf", [128, 128], "bfloat16"),
    "cB": ("sbuf", [128, 256], "bfloat16"), "cQ": ("sbuf", [128, 256], "bfloat16"),
    "khi": ("sbuf", [128, 32], "bfloat16"), "klo": ("sbuf", [128, 32], "bfloat16"),
    "pi": ("sbuf", [128, 1], "int32"), "pa": ("sbuf", [128, 1], "int32"), "pg": ("sbuf", [128, 1], "int32"),
    "p15": ("sbuf", [128, 1], "float32"), "pgf": ("sbuf", [128, 1], "float32"), "k0": ("sbuf", [128, 1], "float32"),
    "kc": ("sbuf", [128, 1], "float32"), "kc2": ("sbuf", [128, 1], "float32"), "kl": ("sbuf", [128, 1], "float32"),
    "cg": ("sbuf", [128, 128], "float32"), "kk": ("sbuf", [128, 16], "float32"), "K16": ("sbuf", [128, 16], "float32"),
    "i16": ("sbuf", [128, 16], "float32"), "il": ("sbuf", [128, 16], "float32"), "i4": ("sbuf", [128, 16], "float32"),
    "ip": ("sbuf", [128, 16], "float32"), "wi": ("sbuf", [128, 1], "int32"), "wf": ("sbuf", [128, 1], "float32"),
}
for _t in range(STEPS):
    SCRATCH["XW%d" % _t] = ("sbuf", [128, 8192 + 256], "bfloat16")
    SCRATCH["ns%d" % _t] = ("sbuf", [128, 16], "float32")
    SCRATCH["na%d" % _t] = ("sbuf", [128, 16], "float32")
    SCRATCH["xs%d" % _t] = ("sbuf", [128, 256], "bfloat16")
for _b in range(8):
    SCRATCH["P%d" % _b] = ("psum", [128, 512], "float32")
SEMAPHORES = ["qV", "qS", "qP", "qG", "loc"] + ["aN%d" % t for t in range(STEPS)] + ["aX%d" % t for t in range(STEPS)] + ["d%d" % j for j in range(12)]


def rank_program(g, core, T, topo):
    rank = T.rank_of(core)
    if rank is None:
        return
    eng = {"V": g.vector, "S": g.scalar, "P": g.tensor, "G": g, "Y": g.sync}
    cnt = {"V": 0, "S": 0, "P": 0, "G": 0, "D": 0, "loc": 0}
    known = {q: {} for q in eng}
    rec = {}
    psum = {"P%d" % b for b in range(8)}
    totals = {}

    def need(q, ev):
        k = known[q]
        if k.get(ev[0], 0) < ev[1]:
            eng[q].wait_ge(T.sem[ev[0]], ev[1])
            for s, v in ev[3].items():
                if k.get(s, 0) < v:
                    k[s] = v
            k[ev[0]] = ev[1]

    def deps(q, dma, reads, writes):
        out = []
        for n, a, b in reads:
            for (c, d, ev, kind) in rec.get(n, ()):
                if n in psum:
                    if ev[2] != q:
                        out.append(ev)
                elif kind == "w" and c < b and a < d:
                    out.append(ev)
        for n, a, b in writes:
            for (c, d, ev, kind) in rec.get(n, ()):
                if n in psum:
                    if ev[2] != q:
                        out.append(ev)
                elif c < b and a < d and (kind == "w" or ev[2] != q):
                    out.append(ev)
        best = {}
        for ev in out:
            if ev[0] not in best or best[ev[0]][1] < ev[1]:
                best[ev[0]] = ev
        for ev in best.values():
            need(q, ev)

    def note(ev, reads, writes):
        for n, a, b in writes:
            if n in psum:
                rec[n] = [(0, 512, ev, "w")]
            else:
                rec[n] = [r for r in rec.get(n, []) if not (a <= r[0] and r[1] <= b)] + [(a, b, ev, "w")]
        for n, a, b in reads:
            if n in psum:
                rec[n] = [(0, 512, ev, "w")]
            else:
                rec[n] = [r for r in rec.get(n, []) if not (r[3] == "r" and r[2][2] == ev[2] and a <= r[0] and r[1] <= b)] + [(a, b, ev, "r")]

    def emit(q, calls, reads, writes):
        deps(q, False, reads, writes)
        last = None
        for c in calls:
            last = c()
        cnt[q] += 1
        last.then_inc(T.sem["q" + q], 1)
        totals["q" + q] = cnt[q]
        note(("q" + q, cnt[q], q, dict(known[q])), reads, writes)

    def dma(q, out, in_, reads, writes):
        deps(q, True, reads, writes)
        s = "d%d" % cnt["D"]
        cnt["D"] += 1
        eng[q].dma_start(out, in_).then_inc(T.sem[s], 16)
        totals[s] = 16
        note((s, 16, "D", dict(known[q])), reads, writes)

    def v(n, a=None, b=None, step=1):
        if a is None:
            a, b = 0, T[n].shape[-1]
        ap = T[n][:, a:b] if step == 1 else T[n][:, a:b:step]
        return (ap, [(n, a, b)])

    def row(n, b):
        return (T[n][0:1, 0:b], [(n, 0, b)])

    def ind(win, off):
        return (win[0].indirect(off[0]), win[1], off[1])

    def split(x):
        return x[1] + (x[2] if len(x) > 2 else [])

    def copy(out, in_):
        emit("V", [lambda: g.vector.tensor_copy(out=out[0], in_=in_[0])], split(in_) + (out[2] if len(out) > 2 else []), out[1])

    def tt(out, a, b, op):
        emit("V", [lambda: g.vector.tensor_tensor(out=out[0], in0=a[0], in1=b[0], op=op)], split(a) + split(b), out[1])

    def ts(out, a, s1, op0, s2=None, op1=None):
        rd = split(a)
        x1, x2 = s1, s2
        if isinstance(s1, tuple):
            rd = rd + s1[1]; x1 = s1[0]
        if isinstance(s2, tuple):
            rd = rd + s2[1]; x2 = s2[0]
        if op1 is None:
            emit("V", [lambda: g.vector.tensor_scalar(out=out[0], in0=a[0], scalar1=x1, scalar2=None, op0=op0)], rd, out[1])
        else:
            emit("V", [lambda: g.vector.tensor_scalar(out=out[0], in0=a[0], scalar1=x1, scalar2=x2, op0=op0, op1=op1)], rd, out[1])

    def fill(out, c):
        emit("V", [lambda: g.vector.memset(out[0], c)], [], out[1])

    def act(out, in_, f, scale=1.0, bias=0.0):
        rd = split(in_)
        sc, bi = scale, bias
        if isinstance(scale, tuple):
            rd = rd + scale[1]; sc = scale[0]
        if isinstance(bias, tuple):
            rd = rd + bias[1]; bi = bias[0]
        emit("S", [lambda: g.scalar.activation(out=out[0], in_=in_[0], func=f, bias=bi, scale=sc)], rd, out[1])

    def mms(items):
        calls, rd, wr = [], [], []
        for o, l, r, a, b in items:
            calls.append(lambda o=o, l=l, r=r, a=a, b=b: g.tensor.matmul(o[0], l[0], r[0], a, b))
            rd = rd + [x for x in l[1] + r[1] if x not in rd]
            wr = wr + [x for x in o[1] if x not in wr]
        emit("P", calls, rd, wr)

    def iota(out, pattern, base, cm, flag=True):
        emit("G", [lambda: g.iota(out[0], pattern, base, cm, allow_small_or_imprecise_dtypes=flag)], [], out[1])

    def asel(out, in_, pattern, op, base, cm, other=0.0):
        emit("G", [lambda: g.affine_select(out[0], in_[0], pattern, op, other, base, cm)], in_[1], out[1])

    def m16(n, r):
        return v(n, 128 * r, 128 * r + 128)

    dma("Y", T.si[:], T.s0[:], [], [("si", 0, 16)])
    dma("S", T.S[:, DUMP + 1024:DUMP + 2048], T.stm[:, 1024:2048], [], [("S", DUMP + 1024, DUMP + 2048)])
    dma("Y", T.wi[:], T.wt[:], [], [("wi", 0, 1)])
    dma("Y", T.S[:, DUMP:DUMP + 1024], T.stm[:, 0:1024], [], [("S", DUMP, DUMP + 1024)])
    dma("Y", T.X[:, XB0:XB0 + V], T.vx[:], [], [("X", XB0, XB0 + V)])
    dma("Y", T.X[:, XB0 + V:XB0 + 2 * V], T.vx[:], [], [("X", XB0 + V, XB0 + 2 * V)])
    dma("Y", T.XW0[:, 0:256], T.x0[:], [], [("XW0", 0, 256)])

    iota(v("pi"), [[0, 1]], 0, 1, False)
    fill(v("onesb"), 1.0)
    iota(v("cg"), [[1, 8], [0, 16]], 0, 0)
    iota(v("kk"), [[1, 16]], 0, 0)
    asel(v("Ib"), v("onesb"), [[-1, 128]], A.is_equal, 0, 1)
    asel(v("Jb"), v("onesb"), [[-2, 64], [1, 2]], A.is_equal, -1, 1)
    ts(v("pa"), v("pi"), 15, A.bitwise_and)
    ts(v("pg"), v("pi"), 4, A.arith_shift_right)
    copy(v("p15"), v("pa"))
    copy(v("pgf"), v("pg"))
    ts(v("blk"), v("cg"), v("pgf"), A.is_equal)
    ts(v("K16"), v("kk"), v("p15"), A.is_equal)
    for k in range(16):
        act(m16("Eb", k), v("Jb"), F.Copy, v("K16", k ^ 1, (k ^ 1) + 1))
    fill(v("Lq"), 0.0)
    fill(v("cB"), -BIG)
    for k in range(16):
        ts(m16("Ea", k), v("Ib"), v("K16", k, k + 1), A.mult)
    fill(v("L"), 0.0)
    copy(v("sl16"), v("si"))
    copy(v("wf"), v("wi"))
    asel(v("tr"), v("blk"), [[1, 128]], A.is_gt, 0, -1)
    iota(v("i16"), [[16, 16]], 0, 0)
    iota(v("khi"), [[0, 2], [256, 16]], 0, 0)
    asel(v("Lp"), v("Lq"), [[-1, 16], [-16, 8], [0, 16]], A.not_equal, 0, 1, -32.0)
    asel(v("Tr"), v("Lq"), [[-1, 16], [-16, 8], [0, 16]], A.is_ge, 0, 1, 1.0)
    asel(v("Tq"), v("Tr"), [[0, 16], [-16, 8], [0, 16]], A.is_ge, 0, 1)
    for r in range(16):
        act(v("L", 128 * r + r, 128 * r + 128, 16), v("blk", r, 128, 16), F.Copy)
    act(v("Wm"), v("L"), F.Copy, v("wf"))
    ts(v("k0"), v("p15"), 0.0, A.is_equal)
    ts(v("kc"), v("p15"), 1.0, A.add, 1.0 / 8192, A.mult)
    ts(v("kc2"), v("kc"), -2.0, A.mult)
    ts(v("kl"), v("p15"), 16.0, A.mult, -1.0, A.add)
    ts(v("il"), v("i16"), v("p15"), A.add)
    ts(v("i4"), v("il"), 4.0, A.mult)
    ts(v("ip"), v("il"), -255.0, A.add)
    ts(v("cF"), v("cB"), 0.0, A.mult, -HALF, A.add)
    ts(v("klo"), v("khi"), 0.0, A.mult, v("kl"), A.add)
    tt(v("Y1"), v("Ib"), v("tr"), A.subtract)
    tt(v("Y2"), v("Y1"), v("Ib"), A.add)
    fill(v("cQ"), -0.25)
    fill(v("c32"), 32.0)
    act(v("I5"), v("Ib"), F.Copy, 5.0)
    act(v("I32"), v("Ib"), F.Copy, 32.0)
    act(v("Ih"), v("Ib"), F.Copy, 0.5)
    act(v("In"), v("Ib"), F.Copy, -1.0)
    act(v("Q1"), v("Y1"), F.Copy, BIG)
    act(v("Q2"), v("Y2"), F.Copy, BIG)
    act(v("LK"), v("L"), F.Copy, v("kc"))
    ts(v("LK2"), v("L"), v("kc2"), A.mult)

    Sw = v("S", DUMP, DUMP + W)
    Xw = v("X", XB0, XB0 + 2 * V)
    starts = [sum(CHUNKS[:j]) for j in range(len(CHUNKS) + 1)]
    later_v, later_s = [], []

    def lists(bank, a, n, mat, src, s0, s1, start=True, stop=True):
        mms([(v(bank, a, a + n), m16(mat, r), v(src, s0 + r, s1, 16), start and r == 0, stop and r == 15) for r in range(16)])

    for t in range(STEPS):
        last = t == STEPS - 1
        h = 1 + t % 3
        XW = "XW%d" % t
        copy(v("c16"), ind(Sw, v("sl16")))

        def gath(j):
            i0, i1 = starts[j], starts[j + 1]
            copy(v("G", 16 * i0, 16 * i1), ind(Sw, v("c16", i0, i1)))

        def sel(j):
            i0, i1 = starts[j], starts[j + 1]
            n = i1 - i0
            b = "P%d" % (j % 2)
            mms([(v(b, n, 2 * n), m16("Eb", k), v("G", 16 * i0 + k, 16 * i1, 16), k == 0, k == 15) for k in range(16)])
            mms([(v(b, 0, n), m16("Ea", k), v("G", 16 * i0 + k, 16 * i1, 16), k == 0, k == 15) for k in range(16)])

        def conv(j):
            i0, i1 = starts[j], starts[j + 1]
            copy(v("lab", 2 * i0, 2 * i1), v("P%d" % (j % 2), 0, 2 * (i1 - i0)))

        def load_b(j):
            i0, i1 = starts[j], starts[j + 1]
            act(v("XB", 16 * i0, 16 * i1), ind(Xw, v("lab", i0 + i1, 2 * i1)), F.Copy)

        def load_a(j):
            i0, i1 = starts[j], starts[j + 1]
            act(v("D", 16 * i0, 16 * i1), ind(Xw, v("lab", 2 * i0, i0 + i1)), F.Copy)
            for q in range(16 * i0, 16 * i1, 512):
                e = min(q + 512, 16 * i1)
                b = ("P6", "P7")[(q - 16 * i0) // 512 % 2]
                mms([(v(b, 0, e - q), v("Ib"), v("D", q, e), True, False), (v(b, 0, e - q), v("In"), v("XB", q, e), False, True)])

        def size_p(j):
            i0, i1 = starts[j], starts[j + 1]
            for q in range(16 * i0, 16 * i1, 512):
                e = min(q + 512, 16 * i1)
                act(v("Z", q, e), v(("P6", "P7")[(q - 16 * i0) // 512 % 2], 0, e - q), F.Abs)

        def size(j):
            i0, i1 = starts[j], starts[j + 1]
            act(v("Z", 16 * i0, 16 * i1), v("D", 16 * i0, 16 * i1), F.Abs)

        def weigh(j, fin=False):
            i0, i1 = starts[j], starts[j + 1]
            mms([(v("P2", i0, i1), m16("Wm", k), v("Z", 16 * i0 + k, 16 * i1, 16), False, fin and k == 15) for k in range(16)])

        def diff(j):
            i0, i1 = starts[j], starts[j + 1]
            tt(v("D", 16 * i0, 16 * i1), ind(Xw, v("lab", 2 * i0, i0 + i1)), v("XB", 16 * i0, 16 * i1), A.subtract)

        gath(0)
        sel(0)
        if later_v:
            later_v[0]()
        else:
            ts(v("c16p"), v("c16"), 1.0, A.add)
            ts(v("sA"), v("si"), 7.0, A.subtract)
        n = len(CHUNKS)
        for j in range(1, n):
            gath(j)
            sel(j)
            conv(j - 1)
            load_b(j - 1)
            if j == 1:
                for f in later_v[1:]:
                    f()
            if j == 2:
                for f in later_s:
                    f()
                mms([(v("P2", 0, 256), row("onesb", 128), row("cF", 256), True, False)])
                mms([(v("P3", 0, 256), v("I32"), v("c16p"), True, False)] +
                    ([(v("P3", 0, 256), v("gB"), v("c32"), False, False)] if t else []) +
                    [(v("P3", r, 256, 16), m16("Lp", r), v("sA"), False, r == 15) for r in range(16)])
                mms([(v("P4", 0, 256), v("Ib"), v("c16p"), True, False), (v("P4", 0, 256), row("onesb", 128), row("cB", 256), False, False)])
                mms([(v("P5", 0, 256), v("Ib"), v("c16p"), True, False)])
        diff(0)
        conv(n - 1)
        load_b(n - 1)
        m = n
        if SONLY:
            m = n - 1
            load_a(m)
        for j in range(m):
            if j + 1 < m:
                diff(j + 1)
            size(j)
            weigh(j, j == m - 1)
            if j == SPOS and SONLY:
                size_p(m)
                weigh(m)
        ts(v("N1"), v("P2", 0, 256), M2K, A.add, M2K, A.subtract)
        tt(v("uq"), v("P2", 0, 256), v("N1"), A.subtract)
        act(v("sq"), v("uq"), F.Square, 1.0, HALF + 16.0)
        ts(v("uh"), v("uq"), HALF, A.add)
        mms([(v("P2", 0, 256), v("Ib"), v("uh"), True, False)])
        tt(v("Qi"), v("sq"), v("P3", 0, 256), A.add)
        ts(v("Qa"), v("Qi"), 480, A.bitwise_and)
        ts(v("cl"), v("Qa"), 0.0, A.is_equal)
        mms([(v("P5", 0, 256), v("Q1"), v("cl"), False, True)])
        mms([(v("P4", 0, 256), v("Q2"), v("cl"), False, True)])
        mms([(v("P6", 0, 256), v("Y1"), v("cl"), True, True), (v("P6", 256, 512), v("Y2"), v("cl"), True, True)])
        act(v("SF"), v("P6", 0, 512), F.Relu, 8192.0)
        mms([(v("P2", 0, 256), v("Q1"), v("cl"), False, True)])
        ts(v("FH", 768, 1024), v("uq"), HALF, A.add, v("k0"), A.mult)
        ts(v("FH", 0, 256), v("P5", 0, 256), -BIG, A.add, 0.0, A.max)
        mms([(v("P3", 0, 256), v("blk"), v("FH", 0, 256), True, True)])
        ts(v("FH", 256, 512), v("P4", 0, 256), 0.0, A.max, 2048.0, A.min)
        lists("P7", 0, 32, "L", "FH", 0, 512)
        copy(v("R1"), v("P3", 0, 256))
        ts(v("FH", 512, 768), v("P2", 0, 256), -BIG, A.add, 0.0, A.max)
        lists("P5", 0, 32, "L", "FH", 512, 1024, True, False)
        mms([(v("P5", 16, 32), v("I5"), v("sA"), False, True)])
        ts(v("c1L"), v("P7", 0, 16), -1.0, A.add)
        ts(v("gl"), v("P7", 16, 32), 2048.0, A.is_gt, 4095.0, A.mult)
        ns, na, xs = "ns%d" % t, "na%d" % t, "xs%d" % t
        tt(v(ns), v("gl"), v("P7", 16, 32), A.add)
        act(v("nb"), v("P7", 0, 16), F.Copy, -1.0)
        dst = T.cores[(rank + h) % len(T.cores)]
        rid, pid = topo.addr(dst, core)
        es = topo.engines(core, dst)[:8]
        mask = sum(1 << e for e in es)
        src = T.cores[(rank - h) % len(T.cores)]
        ein = len(topo.engines(src, core)[:8])

        def send(buf, out, n, sem):
            deps("G", True, [(buf, 0, n)], [])
            g.remote_dma(out, T[buf][:], T.sem[sem], T.sem.loc, pid, rid, mask)
            cnt["loc"] += len(es)
            totals["loc"] = cnt["loc"]
            totals[sem] = ein

        send(ns, T[na][:], 16, "aN%d" % t)
        mms([(v("P0", 0, 32), v("Ib"), v("khi"), True, False), (v("P0", 0, 32), v("Ib"), v("klo"), False, False)] +
            [(v("P0", 0, 32), m16("LK", r), v("SF", r, 512, 16), False, False) for r in range(16)] +
            [(v("P0", 16, 32), m16("LK2", r), v("SF", r, 256, 16), False, r == 15) for r in range(16)])
        for q in range(Q0):
            ts(v("EQ", 272 * q, 256 * q + 256), v("R1", 16 * q, 256), v("c1L", q, q + 1), A.subtract, 1.0, A.is_equal)
        copy(v("zo16"), v("P0", 0, 32))
        for q in range(Q0, 16):
            n = EW * (q - Q0)
            act(v("EA", n, n + EW), v("P3", 16 * Q0, 256), F.Abs, 1.0, v("nb", q, q + 1))
        act(v("EB"), v("EA"), F.Relu, -1.0, 1.0)
        act(v("zz"), ind(v("Z"), v("zo16")), F.Copy)
        mms([(v("P6", 0, 256), m16("Tq", 0), v("EQ", 0, 256), True, False)] +
            [(v("P6", 16 * (q + 1), 256), v("blk"), v("EQ", 272 * q + 16, 256 * (q + 1)), False, False) for q in range(Q0)] +
            [(v("P6", r, 16 * Q0, 16), m16("Tq", r), v("EQ", r, 272 * Q0 - 16, 272), False, False) for r in range(1, 16)])
        mms([(v("P6", 16 * (q + 1), 256), v("blk"), v("EB", EW * (q - Q0) + 16 * (q - Q0 + 1), EW * (q - Q0 + 1)), False, False) for q in range(Q0, 15)] +
            [(v("P6", 16 * Q0 + r, 256, 16), m16("Tq", r), v("EB", r, EW * (16 - Q0), EW + 16), False, r == 15) for r in range(1, 16)])
        mms([(v("P4", 0, 256), v("Ib"), v(XW, 0, 256), True, False), (v("P4", 0, 256), v("In"), v("zz", 256, 512), False, True)])
        mms([(v("P4", 256, 512), v("Ih"), v(XW, 0, 256), True, False), (v("P4", 256, 512), v("Ih"), v("zz", 0, 256), False, False),
             (v("P4", 256, 512), row("onesb", 128), row("cQ", 256), False, True)])
        act(v("cnr"), v("P6", 0, 256), F.Copy, -8192.0)
        act(v(xs), v("P4", 0, 256), F.Abs)
        act(v("N1"), v("P4", 256, 512), F.Identity, 1.0, MAGIC)
        send(xs, T[XW][:, 4096:4352], 256, "aX%d" % t)
        act(v(XW, 8192, 8448), v("N1"), F.Identity, 1.0, -MAGIC)
        if not last:
            emit("S", [lambda: g.scalar.activation(out=T.gf[:], in_=T.gl[:], func=F.Sign, accum_out=T.gs[:])], [("gl", 0, 16)], [("gf", 0, 16), ("gs", 0, 1)])
            act(v("gB"), v("onesb"), F.Copy, v("gs"))
        copy(v("cl16"), v("c1L"))
        ts(v("hs"), v("c1L"), 0.0, A.is_ge, 8192.0, A.mult)
        ts(v("w1"), v("P5", 16, 32), 35.0, A.add)
        tt(v("c1P"), v("c1L"), v("hs"), A.add)
        tt(v("ux"), v("hs"), v("P5", 0, 16), A.add)
        ts(v("c1h"), v("c1P"), -8191.0, A.add)
        tt(v("nc"), ind(Sw, v("cl16")), v("FH", 512, 768), A.add)
        ts(v("w2"), v("w1"), 2047, A.bitwise_and)
        ts(v("nd"), v("nc"), 2047, A.bitwise_and)
        ts(v("w3"), v("w2"), 2048.0, A.add)
        tt(v("b0"), v("w3"), v("c1P"), A.max)
        mms([(v("P3", 0, 16), v("Ib"), v("c1h"), True, False)] +
            [(v("P3", 0, 16), m16("Ea", r), v("cnr", r, 256, 16), False, r == 15) for r in range(16)])
        ts(v("uy"), v("ux"), 8195, A.bitwise_and)
        tt(v("xo"), v("uy"), v("i4"), A.add)
        copy(v("xo16"), v("xo"))
        copy(ind(v("X", 0, XB0 + V), v("xo16")), v("zz", 0, 256))
        tt(v("so"), v("ip"), v("P3", 0, 16), A.max)
        ts(v("so16"), v("so"), 255.0, A.add)
        copy(ind(v("S"), v("so16")), v("nd"))

        def write_x():
            ts(v("c16p"), v("c16"), 1.0, A.add)
            ts(v("sA"), v("si"), 7.0, A.subtract)
            copy(ind(v("X", V, XB0 + 2 * V), v("xo16")), v("zz", 0, 256))

        if last:
            for j in range(2):
                copy(v("G", 1024 * j, 1024 * j + 1024), v("S", DUMP + 1024 * j, DUMP + 1024 * j + 1024))
                mms([(v("P0", 0, 256), v("Ib"), v("G", 1024 * j + 256 * q, 1024 * j + 256 * q + 256), j == 0 and q == 0, j == 1 and q == 3) for q in range(4)])
            act(v("yto"), v("P0", 0, 256), F.Copy)
            dma("Y", T.yv[:], T.X[:, XB0:XB0 + V], [("X", XB0, XB0 + V)], [])
            dma("Y", T.yt[:], T.yto[:], [("yto", 0, 256)], [])
        rec[na] = [(0, 16, ("aN%d" % t, ein, "R", {}), "w")]
        tt(v("vi"), v("b0"), v(na), A.max)
        ts(v("si"), v("vi"), 2047, A.bitwise_and)
        copy(v("sl16"), v("si"))

        def selx(t=t):
            ts(v("sx"), v("vi"), 12288, A.bitwise_and)
            tt(v("sy"), v("sx"), v("il"), A.add)
            copy(v("sel16"), v("sy"))

        def newx(t=t, last=last, ein=ein):
            rec["XW%d" % t] = rec["XW%d" % t] + [(4096, 4352, ("aX%d" % t, ein, "R", {}), "w")]
            act(v("XF") if last else v("XW%d" % (t + 1), 0, 256), ind(v("XW%d" % t), v("sel16")), F.Copy)

        if not last:
            later_v = [write_x, selx]
            later_s = [newx]
        else:
            copy(v("yso"), v("si"))
            dma("Y", T.ys[:], T.yso[:], [("yso", 0, 16)], [])
            selx()
            newx()
            dma("S", T.yx[:], T.XF[:], [("XF", 0, 256)], [])
    for s, n in totals.items():
        g.sync.wait_ge(T.sem[s], n)
